import numpy as np, ml_dtypes
CORES = [25,29,65,69,153,157,193,197]
N = 8
import mx_ref
BF = ml_dtypes.bfloat16
def pick(q, e):
    c = np.concatenate([q[0].reshape(128, -1, 4), np.zeros((128, 1, 4), np.uint8)], axis=1); s = np.concatenate([q[1], np.ones((16, 1), np.uint8)], axis=1)
    return (np.ascontiguousarray(c[:, e].reshape(128, -1)), np.ascontiguousarray(s[:, e]))
def join(*qs):
    return (np.concatenate([q[0] for q in qs], axis=1), np.concatenate([q[1] for q in qs], axis=1))
def put(q, e, v):
    c, s = q[0].reshape(128, -1, 4).copy(), q[1].copy(); c[:, e] = v[0].reshape(128, -1, 4); s[:, e] = v[1]
    return (c.reshape(128, -1), s)
def pk(c, s):
    return (np.ascontiguousarray(c), mx_ref.live(s))
def emit(q):
    return q[0], q[1]
def decode(q):
    o = []
    for b in range(4):
        e = np.zeros((128, 128, 4), np.float32); e[np.arange(128), np.arange(128), b] = 1
        o.append(mx_ref.matmul(mx_ref.quantize(e.reshape(128, 512).astype(BF)), q))
    return np.stack(o, axis=2).reshape(128, -1)
def f(rng, *shape):
    return mx_ref.flush((rng.standard_normal(shape, dtype=np.float32) * np.exp2(rng.integers(-2, 3, shape[:-1] + (1,)))).astype(BF))
def wide(rng, *shape, cols=0):
    v = rng.standard_normal(shape, dtype=np.float32) * np.exp2(rng.integers(-12, 13, shape)).astype(np.float32)
    if cols: v *= np.repeat(np.exp2(rng.integers(-cols, cols + 1, shape[:-2] + (1, shape[-1] // 4))) * (rng.random(shape[:-2] + (1, shape[-1] // 4)) > 0.0625), 4, axis=-1).astype(np.float32)
    return mx_ref.flush(v.astype(BF))
P, C, G, H = 64, 128, 16, 3
F = 96
def trim(v):
    v = v.astype(np.float32)
    v[np.abs(v) < np.float32(2.0 ** -20)] = 0
    return v.astype(BF)
def alike(v):
    return np.stack([v] * N).astype(np.float32).astype(BF)
def flat(v):
    return v.reshape(N, 128, -1).astype(np.float32).astype(BF)
def planted(rng, sign, m, a, b):
    v, t = 1 + rng.random((N, 128, P, 4)), 1 + rng.random((N, 128, C, 4))
    if sign < 0:
        v = 64.0 * (1 + (np.argsort(v, axis=-1) < 2))
        t[:] = 4
    for r in range(N):
        if sign < 0: v[r, m[r], np.arange(P)] = 128
        else: v[r, m[r], np.arange(P)] *= 64
        at = rng.permutation(np.arange(C) % F)
        g = np.zeros(C)
        if sign > 0:
            g[:] = 4
            o = rng.permutation(C)
            g[o[np.unique(at[o], return_index=True)[1]]] = 16
        t[r, at, np.arange(C)] *= g[:, None]
        t[r, :F] *= 2.0 ** 25 if sign < 0 else 2.0 ** 20
        t[r, F:] = 0
        t[r, F + 16:] = -b[r, at][None, :, None] * 2.0 ** 24
    v *= sign * 2.0 ** 20
    v[:, F:] = 0
    v[:, F:F + 16] = -a[:, None, :, None] * 2.0 ** 24
    u = np.zeros((128, 4))
    u[F:] = 2.0 ** 29
    return {"pn": flat(v), "x": flat(t), "u": alike(u), "w": f(rng, N, 128, 512)}
def setup_inputs(rng):
    return {"pn": trim(f(rng, N, 128, 4 * P)), "x": trim(f(rng, N, 128, 4 * C)), "u": alike(f(rng, 128, 4)), "w": f(rng, N, 128, 512)}
def setup_inputs_near(rng):
    K = min(P, C // 2)
    z = rng.integers(4, 8, (128, K, 4)) * rng.choice([-1.0, 1.0], (128, K, 4))
    z[:16] = 0
    u = rng.integers(4, 8, (128, 4)) * rng.choice([-1.0, 1.0], (128, 4))
    u[:16] = 0
    u[8, 0] = 2.0 ** -8
    v, t = np.zeros((N, 128, P, 4)), np.zeros((N, 128, C, 4))
    for r in range(N):
        v[r] = z[:, rng.permutation(np.arange(P) % K)]
        v[r, 0, :, 0] = 2.0 ** -4
        at = rng.permutation(np.arange(C) % K)
        small = np.ones(C)
        for k in range(K):
            e = np.flatnonzero(at == k)
            if k % 3 == 0: small[e[-1]] = 2
            if k % 3 == 2: small[e[0]] = 2
        more = np.full(K, -1.0)
        o = rng.permutation(K)
        more[o[:K // 2]] = 1
        more[o[K // 2:K // 2 + K // 4]] = 0
        t[r] = z[:, at]
        t[r, 0, :, 0] = small * 2.0 ** -4
        t[r, 8, :, 0] = more[at] * 2.0 ** -4
    g = 2.0 ** -int(rng.integers(12, 17))
    return {"pn": flat(v * g), "x": flat(t * g), "u": alike(u * 2.0 ** -int(rng.integers(12, 21))), "w": f(rng, N, 128, 512)}
def setup_inputs_below(rng):
    m, b = np.stack([rng.permutation(F)[:P] for r in range(N)]), np.full((N, F), 4.0)
    for r in range(N): b[(r + 1) % N, m[r, rng.permutation(P)[:2 * G]]] = 1
    return planted(rng, -1, m, np.full((N, P), 2.0), b)
def setup_inputs_crowd(rng):
    E = P // 2
    n = rng.permutation(np.array([G, 0, G + 1, G - 1, 1, E, G, G + 1])[:N])
    m, a = np.zeros((N, P), int), np.full((N, P), 8.0)
    for r in range(N):
        g = rng.permutation(np.arange(P) % E)
        m[r] = rng.permutation(F)[g]
        a[r, np.unique(g, return_index=True)[1][rng.permutation(E)[n[r]:]]] = 2
    return planted(rng, 1, m, a, np.full((N, F), 4.0))
def setup_inputs_spread(rng):
    return {**setup_inputs(rng), "pn": trim(wide(rng, N, 128, 4 * P, cols=6)), "x": trim(wide(rng, N, 128, 4 * C, cols=6))}
def check_inputs(d):
    b = []
    for k, lo, hi in (("pn", -20, 27), ("x", -20, 27), ("u", -30, 30), ("w", -30, 30)):
        v = np.abs(d[k].astype(np.float32))
        if not (np.isfinite(v).all() and ((v == 0) | (v >= 2.0 ** lo) & (v <= 2.0 ** hi)).all()): b.append("a value of " + k)
    v = d["u"].astype(np.float32)
    if not (v == v[:1]).all(): b.append("u differs between ranks")
    return b
def upto(e, n):
    return np.concatenate([e, np.full(n - len(e), -1)])
def visit(a, b, k):
    s = mx_ref.matmul(pick(a, upto(np.arange(P), 128)), b)[:P] + np.float32(0)
    place = np.argmax(s, axis=1)
    v = mx_ref.matmul(k, join(a, b))[0] + np.float32(0)
    owns = np.zeros(P, bool)
    owns[np.unique(place, return_index=True)[1]] = True
    i = np.flatnonzero(owns & (v[P + place] > v[:P]))[:G]
    if len(i) == 0: return a, b
    j = place[i]
    d = decode(join(pick(a, upto(i, G)), pick(b, upto(j, G))))
    z = mx_ref.quantize(np.ascontiguousarray((d[:, :4 * G] - np.float32(0.5) * d[:, 4 * G:]).astype(BF)))
    return put(a, i, pick(b, j)), put(b, j, pick(z, np.arange(len(i))))
def reference(pn, x, u, w):
    a = [mx_ref.quantize(np.ascontiguousarray(pn[r])) for r in range(N)]
    b = [mx_ref.quantize(np.ascontiguousarray(x[r])) for r in range(N)]
    k = [mx_ref.quantize(np.concatenate([u[r], np.zeros((128, 508), BF)], axis=1)) for r in range(N)]
    wq = [mx_ref.quantize(np.ascontiguousarray(w[r])) for r in range(N)]
    y = np.zeros((N, 128, H * P), np.float32)
    for h in range(H):
        a = [a[r - 1] for r in range(N)]
        for r in range(N):
            a[r], b[r] = visit(a[r], b[r], k[r])
            y[r, :, h * P:h * P + P] = mx_ref.matmul(wq[r], a[r])
    p, t = [emit(v) for v in a], [emit(v) for v in b]
    return {"y": y, "pc": np.stack([v[0] for v in p]), "psc": np.stack([v[1] for v in p]), "oc": np.stack([v[0] for v in t]), "osc": np.stack([v[1] for v in t])}

@@ -1,0 +1,310 @@
+from concourse.bass import DstId, RemoteDMATransfer
+from concourse.mybir import dt, AluOpType, ActivationFunctionType
+
+P, C, G, H = 64, 128, 16, 3
+X4, U8, BF, F32 = "float8_e4m3fn_x4", "uint8", "bfloat16", "float32"
+PN0, FP0, FM0, Z0, Q0, X10, WC0, WM0, CBW = 0, 256, 776, 1296, 1552, 1808, 2320, 2832, 3344
+SRC = [("k0", 0), ("k1", 128), ("k2", 128), ("k3", 512)]
+PAD = 256
+
+SCRATCH = {
+    "cb": ("sbuf", [128, CBW], BF), "xt": ("sbuf", [128, 512], BF), "wt": ("sbuf", [128, 512], BF),
+    "ut": ("sbuf", [128, 8], BF), "ur": ("sbuf", [128, 512], BF), "tt": ("sbuf", [128, 512], BF),
+    "di": ("sbuf", [128, 128], F32), "d16": ("sbuf", [128, 128], F32), "pi": ("sbuf", [128, 4], "int32"),
+    "pj": ("sbuf", [128, 4], "int32"), "pf": ("sbuf", [128, 4], F32), "iot": ("sbuf", [128, 64], F32),
+    "inv": ("sbuf", [128, 576], F32), "tmp": ("sbuf", [128, 128], F32), "dp": ("sbuf", [128, 64], F32),
+    "dt1": ("sbuf", [128, 128], F32), "dt2": ("sbuf", [128, 128], F32), "hh": ("sbuf", [128, 128], F32),
+    "up": ("sbuf", [128, 4], F32), "pmx": ("sbuf", [128, 128], F32), "cc": ("sbuf", [128, 64], F32),
+    "mm": ("sbuf", [128, 64], F32), "st": ("sbuf", [128, 64], F32), "stt": ("sbuf", [128, 128], F32),
+    "offp": ("sbuf", [128, 16], "uint16"), "offt": ("sbuf", [128, 32], "uint16"), "yy": ("sbuf", [128, 192], F32),
+    "pa": ("psum", [128, 512], F32), "pb": ("psum", [128, 512], F32), "pcc": ("psum", [128, 512], F32),
+    "pd": ("psum", [128, 512], F32),
+}
+for _b in range(4):
+    SCRATCH["pz%d" % _b] = ("psum", [128, 512], F32)
+for _n, _w, _ws in (("k0", 256, 256), ("k1", 448, 448), ("k2", 448, 448), ("k3", 576, 576), ("wq", 128, 128),
+                    ("uq", 128, 128), ("tq", 128, 128), ("qq", 128, 128), ("w1", 320, 512), ("w2", 320, 512),
+                    ("w3", 320, 512), ("w4", 256, 256), ("r1", 64, PAD), ("r2", 64, PAD), ("r3", 64, PAD)):
+    SCRATCH[_n + "c"] = ("sbuf", [128, _w], X4)
+    SCRATCH[_n + "s"] = ("sbuf", [128, _ws], U8)
+
+SEMAPHORES = ["lpn", "lx", "lu", "lw", "g1", "g2", "g3", "g4", "a1", "a2", "a3", "a4", "qpn", "qx", "qu", "b1", "b2", "b3",
+              "b4", "qe", "s1", "s2", "arr1", "arr2", "arr3", "rl1", "rl2", "rl3", "sent",
+              "tu", "ts", "tr", "tv", "tc", "tm", "tz0", "tz1", "tz2", "tz3", "ty",
+              "vs", "vt", "vq1", "vq", "vq2", "vc", "vm", "vg", "vo", "va", "vi", "vst", "vot", "vz", "vqz", "vb",
+              "su", "sh", "sa", "sz", "sy", "sb", "st1", "st2"]
+
+
+def _mask(engines):
+    m = 0
+    for e in engines:
+        m |= 1 << e
+    return m
+
+
+def _relays(topo, src, dst, cores):
+    c = [k for k in topo.cores_of(src) if k not in cores and topo.may_write(k, dst)]
+    c = [k for k in c if topo.die(k) == topo.die(src)] + [k for k in c if topo.die(k) != topo.die(src)]
+    return c[:2]
+
+
+def _first_hop(topo, src, dst, cores, s):
+    if topo.may_write(src, dst):
+        e = topo.engines(src, dst)
+        return (dst, e[0::2]), (dst, e[1::2])
+    a, b = _relays(topo, src, dst, cores)
+    ea, eb = topo.engines(src, a), topo.engines(src, b)
+    if s == 1:
+        return (a, ea[0::4]), (b, eb[2::4])
+    return (a, ea[0::2]), (b, eb[1::2])
+
+
+def _second_hop(topo, relay, dst, s):
+    return topo.engines(relay, dst)
+
+
+def _arrival(topo, src, dst, cores, s):
+    if topo.may_write(src, dst):
+        (a, ea), (b, eb) = _first_hop(topo, src, dst, cores, s)
+        return len(ea) + len(eb)
+    return sum(len(_second_hop(topo, k, dst, s)) for k in _relays(topo, src, dst, cores))
+
+
+def relay_program(g, core, T, topo):
+    cores = list(T.cores)
+    n = len(cores)
+    for r in range(n):
+        src, dst = cores[r], cores[(r + 1) % n]
+        if topo.may_write(src, dst):
+            continue
+        rel = _relays(topo, src, dst, cores)
+        if core not in rel:
+            continue
+        role = rel.index(core)
+        rid, pid = topo.addr(dst, core)
+        sent = 0
+        for s in range(1, H + 1):
+            g.wait_ge(T.sem["rl%d" % s], len(_first_hop(topo, src, dst, cores, s)[role][1]))
+            e = _second_hop(topo, core, dst, s)
+            if role == 0:
+                o, i = T["w%dc" % s][:, 256:320].bitcast(dt.uint8), T["r%dc" % s][:, 0:P].bitcast(dt.uint8)
+            else:
+                o, i = T["w%ds" % s][:, 256:320], T["r%ds" % s][:, 0:P]
+            g.remote_dma(o, i, T.sem["arr%d" % s], T.sem.sent, pid, rid, _mask(e))
+            sent += len(e)
+        g.wait_ge(T.sem.sent, sent)
+
+
+def rank_program(g, core, T, topo):
+    rank = T.rank_of(core)
+    if rank is None:
+        relay_program(g, core, T, topo)
+        return
+    cores = list(T.cores)
+    n = len(cores)
+    nxt, prv = cores[(rank + 1) % n], cores[(rank - 1) % n]
+    V, S, E, Y = g.vector, g.scalar, g.tensor, g.sync
+    A, ACT = AluOpType, ActivationFunctionType
+    cnt, seen = {}, {}
+
+    def sig(ins, name, k=1):
+        ins.then_inc(T.sem[name], k)
+        cnt[name] = cnt.get(name, 0) + k
+
+    def w(q, *names):
+        for nm in names:
+            q.wait_ge(T.sem[nm], cnt[nm])
+            seen[nm] = cnt[nm]
+
+    def qz(name, a, b, src):
+        return V.quantize_mx(T[name + "c"][:, a:b], T[name + "s"][:, a:b], src)
+
+    def mm(out, l, la, r, ra, start=True, stop=True):
+        return E.matmul_mx(out[:, 0:128], T[l + "c"][:, la:la + 128], T[l + "s"][:, la:la + 128],
+                           T[r + "c"][:, ra:ra + 128], T[r + "s"][:, ra:ra + 128], start, stop)
+
+    def send(s):
+        name, a0 = SRC[s - 1]
+        (da, ea), (db, eb) = _first_hop(topo, core, nxt, cores, s)
+        direct = da == nxt
+        land, l0, sem = ("w%d" % s, 256, "arr%d" % s) if direct else ("r%d" % s, 0, "rl%d" % s)
+        co, ci = T[land + "c"][:, l0:l0 + P].bitcast(dt.uint8), T[name + "c"][:, a0:a0 + P].bitcast(dt.uint8)
+        (ra, pa), (rb, pb) = topo.addr(da, core), topo.addr(db, core)
+        if direct and s == 1:
+            g.remote_dma(co, ci, T.sem[sem], T.sem.sent, pa, ra, _mask(ea))
+            g.remote_dma(T[land + "s"][:, l0:l0 + P], T[name + "s"][:, a0:a0 + P], T.sem[sem], T.sem.sent, pb, rb, _mask(eb))
+        else:
+            g.remote_dma_fused([
+                RemoteDMATransfer(dst_ids=[DstId(rid=ra, pnc=pa)], dma_engine_mask=_mask(ea), remote_sem=T.sem[sem], src=ci, dst=co),
+                RemoteDMATransfer(dst_ids=[DstId(rid=rb, pnc=pb)], dma_engine_mask=_mask(eb), remote_sem=T.sem[sem],
+                                  src=T[name + "s"][:, a0:a0 + PAD], dst=T[land + "s"][:, l0:l0 + PAD]),
+            ], local_sem=T.sem.sent)
+        cnt["sent"] = cnt.get("sent", 0) + len(ea) + len(eb)
+
+    cb = T.cb
+    sig(Y.dma_start(cb[:, PN0:PN0 + 256], T.pn[:]), "lpn", 16)
+    sig(Y.dma_start(T.xt[:], T.x[:]), "lx", 16)
+    sig(Y.dma_start(T.ut[:, 0:4], T.u[:]), "lu", 16)
+    sig(Y.dma_start(T.wt[:], T.w[:]), "lw", 16)
+    sig(g.iota(T.di[:], [[1, 128]], 0, -1, allow_small_or_imprecise_dtypes=True), "g1")
+    sig(g.iota(T.d16[:], [[0, 8], [1, 16]], 0, -1, allow_small_or_imprecise_dtypes=True), "g2")
+    sig(g.iota(T.pi[:, 0:1], [[0, 1]], 0, 1), "g2")
+    sig(V.memset(cb[:, FP0:FM0], 0.0), "a1")
+    sig(V.memset(T.tt[:], 0.0), "a2")
+    w(V, "g1", "a1")
+    sig(V.tensor_scalar(cb[:, FP0 + 3:FP0 + 515:4], T.di[:], 0.0, None, A.is_equal), "a3")
+    sig(V.memset(cb[:, X10:WM0], 0.0), "a2")
+    w(V, "a3")
+    sig(qz("k0", 128, 256, cb[:, FP0 + 3:FP0 + 515]), "a4")
+    w(V, "lpn")
+    sig(qz("k0", 0, 128, cb[:, PN0:PN0 + 512]), "qpn")
+    w(g, "a4", "qpn")
+    send(1)
+    sig(g.iota(T.iot[:], [[1, 64]], 64, 0, allow_small_or_imprecise_dtypes=True), "g3")
+    sig(g.iota(T.inv[:], [[0, 3], [1, 192]], 128, 0, allow_small_or_imprecise_dtypes=True), "g4")
+    w(S, "g1", "lu")
+    for t in range(4):
+        sig(S.activation(T.ur[:, t:512:4], T.di[:], ACT.Identity, bias=T.ut[:, t:t + 1], scale=0.0), "s1")
+    w(S, "a3")
+    sig(S.activation(cb[:, FM0:Z0], cb[:, FP0:FM0], ACT.Copy, scale=-0.5), "s2")
+    w(V, "lx")
+    sig(qz("w1", 128, 256, T.xt[:]), "qx")
+    w(V, "a2", "g2")
+    d = T.di[64:128, 64:128]
+    sig(V.tensor_scalar(T.tmp[64:128, 0:64], d, 0.0, None, A.is_gt), "b1")
+    sig(V.tensor_scalar(T.tmp[64:128, 64:128], d, 0.0, None, A.is_equal), "b1")
+    sig(V.tensor_scalar(T.pj[:, 0:1], T.pi[:, 0:1], 15, None, A.bitwise_and), "b1")
+    sig(V.tensor_scalar(T.pj[:, 1:2], T.pi[:, 0:1], 112, None, A.bitwise_and), "b1")
+    sig(V.tensor_scalar(cb[64:128, X10 + 4:WC0:8], d, 0.0, None, A.is_equal), "b2")
+    sig(V.memset(cb[0:1, X10:WC0:8], 1.0), "b2")
+    sig(V.memset(T.tt[0:1, 0:512:4], 1.0), "b2")
+    sig(V.memset(T.hh[:, 1:128:2], 0.5), "b2")
+    w(V, "s1")
+    sig(qz("uq", 0, 128, T.ur[:]), "qu")
+    w(V, "b1")
+    sig(V.tensor_tensor(cb[64:128, X10:WC0:8], T.tmp[64:128, 0:64], T.tmp[64:128, 64:128], A.subtract), "b2")
+    sig(V.tensor_tensor(cb[64:128, X10 + 1:WC0:8], T.tmp[64:128, 64:128], T.tmp[64:128, 0:64], A.subtract), "b2")
+    sig(V.tensor_copy(T.pf[:, 0:1], T.pj[:, 0:1]), "b2")
+    sig(V.tensor_scalar(T.pf[:, 1:2], T.pj[:, 1:2], -1.0, None, A.mult), "b2")
+    sig(V.memset(cb[:, WC0:WM0:4], 256.0), "b2")
+    sig(V.memset(cb[:, WM0:CBW:4], -256.0), "b2")
+    sig(V.memset(cb[:, WM0 + 2:CBW:4], 1.0), "b2")
+    sig(V.memset(cb[:, WM0 + 3:CBW:4], 0.0), "b2")
+    sig(V.tensor_scalar(cb[:, WM0 + 1:CBW:4], T.d16[:], 0.0, 512.0, A.is_equal, A.mult), "b2")
+    sig(V.tensor_scalar(cb[:, Q0 + 1:X10:4], T.d16[:, 0:64], 0.0, None, A.not_equal), "b2")
+    sig(V.memset(cb[:, Q0 + 3:X10:4], 0.0), "b2")
+    sig(V.memset(T.dp[:], -1000.0), "b2")
+    w(V, "b2")
+    sig(qz("k1", 0, 128, cb[:, X10:WC0]), "b3")
+    sig(qz("k1", 192, 448, cb[:, WC0:CBW]), "b3")
+    sig(V.tensor_scalar(T.dt1[:], T.d16[:], T.pf[:, 1:2], -1048576.0, A.is_equal, A.mult), "b4")
+    sig(V.tensor_scalar(T.pf[:, 2:3], T.pf[:, 0:1], -1024.0, 15360.0, A.mult, A.add), "b4")
+    w(V, "g3")
+    sig(V.tensor_scalar(T.dp[:, 0:64:16], T.iot[:, 0:64:16], T.pf[:, 0:1], -192.0, A.add, A.add), "b4")
+    EB = [("k0", 128), ("k2", 0), ("k2", 192), ("k2", 320)]
+    for b in range(1, 4):
+        sig(qz(EB[b][0], EB[b][1], EB[b][1] + 128, cb[:, FP0 + 3 - b:FP0 + 515 - b]), "qe")
+    w(V, "s2", "lw")
+    for b in range(4):
+        sig(qz("k3", 128 * b, 128 * b + 128, cb[:, FM0 + 3 - b:FM0 + 515 - b]), "qe")
+    sig(qz("wq", 0, 128, T.wt[:]), "qe")
+    w(V, "b4")
+    sig(V.tensor_scalar(T.dt2[:], T.dt1[:], 1024.0, None, A.add), "qe")
+    w(V, "qe", "g4")
+    zero = cb[:, WC0 + 1:WM0:4]
+    w(E, "qx", "qu")
+
+    for h in range(1, H + 1):
+        Wn, Wx = "w%d" % h, "w%d" % (h + 1)
+        an, a0 = SRC[h]
+        op, ot = T.offp[:, 4 * h:4 * h + 4], T.offt[:, 8 * h:8 * h + 8]
+        iv = 192 * (h - 1)
+        sig(mm(T.pd, Wn, 128, "uq", 0), "tu")
+        w(S, "tu")
+        sig(S.activation(T.up[:, 0:1], T.pd[:, 0:1], ACT.Copy), "su")
+        E.wait_ge(T.sem["arr%d" % h], _arrival(topo, prv, core, cores, h))
+        sig(mm(T.pa, Wn, 192, Wn, 128), "ts")
+        sig(mm(T.pb, "uq", 0, Wn, 192), "tr")
+        w(S, "su", "tr")
+        sig(S.activation(T.hh[:, 0:128:2], T.pb[:, 64:128], ACT.Sign, bias=T.up[:, 0:1], scale=-1.0), "sh")
+        w(V, "ts")
+        sig(V.tensor_tensor_scan(T.pmx[64:128, :], T.pa[64:128, 0:128], cb[64:128, WC0 + 1:WM0:4], -1e29, A.max, A.add), "vs")
+        w(V, "vs")
+        sig(V.tensor_scalar(T.tt[64:128, 0:512:4], T.pmx[64:128, 0:128], T.pmx[64:128, 127:128], None, A.is_ge), "vt")
+        sig(V.tensor_scalar(T.tt[64:128, 5:512:4], T.pmx[64:128, 0:127], T.pmx[64:128, 127:128], None, A.is_ge), "vt")
+        w(V, "vt")
+        sig(qz("tq", 0, 128, T.tt[:]), "vq1")
+        if h == 1:
+            w(E, "b3")
+        w(E, "vq1")
+        sig(mm(T.pcc, "tq", 0, "k1", 0), "tv")
+        w(V, "tv", "sh")
+        sig(V.tensor_tensor(cb[:, Q0:X10:2], T.pcc[:, 0:128], T.hh[:], A.is_lt), "vq")
+        w(V, "vq")
+        sig(qz("qq", 0, 128, cb[:, Q0:Q0 + 512]), "vq2")
+        w(E, "vq2")
+        sig(mm(T.pcc, "k1", 192, "qq", 0), "tc")
+        sig(mm(T.pb, "k1", 320, "qq", 0), "tm")
+        if h == 1:
+            w(E, "a4", "qe")
+        for b in range(4):
+            mm(T["pz%d" % b], EB[b][0], EB[b][1], Wn, 192, True, False)
+        w(V, "tc")
+        sig(V.tensor_tensor_scan(T.cc[:], T.pcc[:, 0:64], cb[:, WC0 + 1:WC0 + 256:4], -256.0 * (G + 1), A.add, A.add), "vc")
+        w(V, "vc", "tm")
+        sig(V.tensor_tensor(T.mm[:], T.pb[:, 0:64], T.cc[:], A.max), "vm")
+        w(V, "vm")
+        sig(V.tensor_tensor_scan(T.st[:], T.dp[:], T.mm[:], -1000.0, A.max, A.min), "vg")
+        w(V, "vg")
+        sig(V.tensor_scalar(op, T.st[:, 15:64:16], 256.0, None, A.add), "vo")
+        w(V, "vo")
+        w(S, "vo")
+        sig(V.tensor_copy(T[an + "c"][:, a0:a0 + P].bitcast(dt.uint32), T[Wn + "c"][:, 128:320].bitcast(dt.uint32).indirect(op)), "va")
+        sig(S.activation(T[an + "s"][:, a0:a0 + P], T[Wn + "s"][:, 128:320].indirect(op), ACT.Copy), "sa")
+        if h < H:
+            w(g, "va", "sa")
+            send(h + 1)
+        sig(V.tensor_copy(T.inv[:, iv:iv + 192].indirect(op), T.iot[:]), "vi")
+        w(E, "va", "sa")
+        for b in range(4):
+            sig(mm(T["pz%d" % b], "k3", 128 * b, an, a0 - 64, False, True), "tz%d" % b)
+        sig(mm(T.pd, "wq", 0, an, a0 - 64), "ty")
+        w(V, "vi")
+        sig(V.tensor_tensor_scan(T.stt[:], T.dt2[:], T.inv[:, iv:iv + 128], 0.0, A.add, A.max), "vst")
+        w(V, "vst")
+        sig(V.tensor_scalar(ot, T.stt[:, 15:128:16], T.pf[:, 2:3], None, A.subtract), "vot")
+        for b in (0, 2):
+            w(S, "tz%d" % b)
+            sig(S.activation(cb[:, Z0 + b:Q0:4], T["pz%d" % b][:, 64:128], ACT.Copy), "sz")
+        for b in (1, 3):
+            w(V, "tz%d" % b)
+            sig(V.tensor_copy(cb[:, Z0 + b:Q0:4], T["pz%d" % b][:, 64:128]), "vz")
+        w(S, "ty")
+        sig(S.activation(T.yy[:, P * (h - 1):P * h], T.pd[:, 64:128], ACT.Copy), "sy")
+        w(V, "vz", "sz")
+        sig(qz(Wn, 0, 128, cb[:, Z0 - 256:Q0]), "vqz")
+        w(V, "vqz", "vot")
+        w(S, "vqz", "vot")
+        sig(V.tensor_copy(T[Wx + "c"][:, 128:256].bitcast(dt.uint32), T[Wn + "c"][:, 0:256].bitcast(dt.uint32).indirect(ot)), "vb")
+        sig(S.activation(T[Wx + "s"][:, 128:256], T[Wn + "s"][:, 0:256].indirect(ot), ACT.Copy), "sb")
+        if h < H:
+            w(E, "sy", "vb", "sb")
+
+    an, a0 = SRC[H]
+    w(Y, "va")
+    sig(Y.dma_start(T.pc[:], T[an + "c"][:, a0:a0 + P].bitcast(dt.uint8)), "st1", 16)
+    w(Y, "sa")
+    for k in range(4):
+        sig(Y.dma_start(T.psc[4 * k:4 * k + 4, :], T[an + "s"][32 * k:32 * k + 4, a0:a0 + P]), "st1", 16)
+    w(Y, "sy")
+    sig(Y.dma_start(T.y[:], T.yy[:]), "st1", 16)
+    w(Y, "vb")
+    sig(Y.dma_start(T.oc[:], T.w4c[:, 128:256].bitcast(dt.uint8)), "st1", 16)
+    w(S, "sb")
+    for k in range(4):
+        sig(S.dma_start(T.osc[4 * k:4 * k + 4, :], T.w4s[32 * k:32 * k + 4, 128:256]), "st2", 16)
+    w(Y, "st1")
+    w(S, "st2")
+    for nm in cnt:
+        if seen.get(nm, 0) < cnt[nm]:
+            w(g, nm)

@@ -1,21 +1,27 @@
 from concourse.bass import DstId, RemoteDMATransfer
-from concourse.mybir import dt, AluOpType, ActivationFunctionType
+from concourse.mybir import dt, AluOpType, AxisListType, ActivationFunctionType
 
 P, C, G, H = 64, 128, 16, 3
 X4, U8, BF, F32 = "float8_e4m3fn_x4", "uint8", "bfloat16", "float32"
-PN0, FP0, FM0, Z0, Q0, X10, WC0, WM0, CBW = 0, 256, 776, 1296, 1552, 1808, 2320, 2832, 3344
+PN0, FP0, FM0, Z0, Q0 = 0, 256, 776, 1296, 1552
 SRC = [("k0", 0), ("k1", 128), ("k2", 128), ("k3", 512)]
+EB = [("k0", 128), ("k2", 0), ("k2", 192), ("k1", 320)]
+FB = [("k2", 320), ("k3", 128), ("k3", 256), ("k3", 384)]
 PAD = 256
 
 SCRATCH = {
-    "cb": ("sbuf", [128, CBW], BF), "xt": ("sbuf", [128, 512], BF), "wt": ("sbuf", [128, 512], BF),
-    "ut": ("sbuf", [128, 8], BF), "ur": ("sbuf", [128, 512], BF), "tt": ("sbuf", [128, 512], BF),
-    "di": ("sbuf", [128, 128], F32), "d16": ("sbuf", [128, 128], F32), "pi": ("sbuf", [128, 4], "int32"),
+    "cb": ("sbuf", [128, Q0], BF), "xt": ("sbuf", [128, 512], BF), "wt": ("sbuf", [128, 512], BF),
+    "ut": ("sbuf", [128, 8], BF), "ur": ("sbuf", [128, 512], BF), "tt": ("sbuf", [128, 520], BF),
+    "x1": ("sbuf", [128, 512], BF), "x2": ("sbuf", [128, 512], BF), "qt": ("sbuf", [128, 512], BF),
+    "ct": ("sbuf", [128, 128], BF), "mt": ("sbuf", [128, 128], BF), "lt": ("sbuf", [128, 128], BF),
+    "l2": ("sbuf", [128, 128], BF), "l3": ("sbuf", [128, 128], BF), "l4": ("sbuf", [128, 128], BF),
+    "di": ("sbuf", [128, 128], F32), "d16": ("sbuf", [128, 128], F32), "dm": ("sbuf", [128, 128], F32),
+    "pi": ("sbuf", [128, 4], "int32"),
     "pj": ("sbuf", [128, 4], "int32"), "pf": ("sbuf", [128, 4], F32), "iot": ("sbuf", [128, 64], F32),
-    "inv": ("sbuf", [128, 576], F32), "tmp": ("sbuf", [128, 128], F32), "dp": ("sbuf", [128, 64], F32),
-    "dt1": ("sbuf", [128, 128], F32), "dt2": ("sbuf", [128, 128], F32), "hh": ("sbuf", [128, 128], F32),
-    "up": ("sbuf", [128, 4], F32), "pmx": ("sbuf", [128, 128], F32), "cc": ("sbuf", [128, 64], F32),
-    "mm": ("sbuf", [128, 64], F32), "st": ("sbuf", [128, 64], F32), "stt": ("sbuf", [128, 128], F32),
+    "inv": ("sbuf", [128, 576], F32), "tmp": ("sbuf", [128, 8], F32), "dp": ("sbuf", [128, 12], F32),
+    "dt2": ("sbuf", [128, 128], F32), "upr": ("sbuf", [128, 128], F32),
+    "nm": ("sbuf", [128, 4], F32), "qf": ("sbuf", [128, 4], F32), "pmx": ("sbuf", [128, 128], F32),
+    "st": ("sbuf", [128, 12], F32), "stt": ("sbuf", [128, 128], F32),
     "offp": ("sbuf", [128, 16], "uint16"), "offt": ("sbuf", [128, 32], "uint16"), "yy": ("sbuf", [128, 192], F32),
     "pa": ("psum", [128, 512], F32), "pb": ("psum", [128, 512], F32), "pcc": ("psum", [128, 512], F32),
     "pd": ("psum", [128, 512], F32),
@@ -23,16 +29,16 @@ SCRATCH = {
 for _b in range(4):
     SCRATCH["pz%d" % _b] = ("psum", [128, 512], F32)
 for _n, _w, _ws in (("k0", 256, 256), ("k1", 448, 448), ("k2", 448, 448), ("k3", 576, 576), ("wq", 128, 128),
-                    ("uq", 128, 128), ("tq", 128, 128), ("qq", 128, 128), ("w1", 320, 512), ("w2", 320, 512),
+                    ("uq", 128, 128), ("tq", 132, 132), ("qq", 128, 128), ("w1", 320, 512), ("w2", 320, 512),
                     ("w3", 320, 512), ("w4", 256, 256), ("r1", 64, PAD), ("r2", 64, PAD), ("r3", 64, PAD)):
     SCRATCH[_n + "c"] = ("sbuf", [128, _w], X4)
     SCRATCH[_n + "s"] = ("sbuf", [128, _ws], U8)
 
-SEMAPHORES = ["lpn", "lx", "lu", "lw", "g1", "g2", "g3", "g4", "a1", "a2", "a3", "a4", "qpn", "qx", "qu", "b1", "b2", "b3",
-              "b4", "qe", "s1", "s2", "arr1", "arr2", "arr3", "rl1", "rl2", "rl3", "sent",
-              "tu", "ts", "tr", "tv", "tc", "tm", "tz0", "tz1", "tz2", "tz3", "ty",
-              "vs", "vt", "vq1", "vq", "vq2", "vc", "vm", "vg", "vo", "va", "vi", "vst", "vot", "vz", "vqz", "vb",
-              "su", "sh", "sa", "sz", "sy", "sb", "st1", "st2"]
+SEMAPHORES = ["lpn", "lx", "lu", "lw", "g1", "g2", "g3", "g4", "a1", "a2", "a3", "qpn", "qx", "qu", "b0", "b1", "b2",
+              "b3", "b4", "qe", "s1", "s2", "arr1", "arr2", "arr3", "rl1", "rl2", "rl3", "sent",
+              "tu", "ts", "tr", "tv", "tm", "tz0", "tz1", "tz2", "tz3", "ty",
+              "vs", "vt", "vq1", "vr", "vq", "vq2", "vg", "vo", "va", "vi", "vst", "vot", "vqz", "vb",
+              "su", "sh", "shi", "slo", "sm", "sa", "sz", "sy", "sb", "st1", "st2"]
 
 
 def _mask(engines):
@@ -48,26 +54,16 @@ def _relays(topo, src, dst, cores):
     return c[:2]
 
 
-def _first_hop(topo, src, dst, cores, s):
+def _first_hop(topo, src, dst, cores):
+    a, b = (dst, dst) if topo.may_write(src, dst) else _relays(topo, src, dst, cores)
+    return (a, topo.engines(src, a)[0::2]), (b, topo.engines(src, b)[1::2])
+
+
+def _arrival(topo, src, dst, cores):
     if topo.may_write(src, dst):
-        e = topo.engines(src, dst)
-        return (dst, e[0::2]), (dst, e[1::2])
-    a, b = _relays(topo, src, dst, cores)
-    ea, eb = topo.engines(src, a), topo.engines(src, b)
-    if s == 1:
-        return (a, ea[0::4]), (b, eb[2::4])
-    return (a, ea[0::2]), (b, eb[1::2])
-
-
-def _second_hop(topo, relay, dst, s):
-    return topo.engines(relay, dst)
-
-
-def _arrival(topo, src, dst, cores, s):
-    if topo.may_write(src, dst):
-        (a, ea), (b, eb) = _first_hop(topo, src, dst, cores, s)
+        (a, ea), (b, eb) = _first_hop(topo, src, dst, cores)
         return len(ea) + len(eb)
-    return sum(len(_second_hop(topo, k, dst, s)) for k in _relays(topo, src, dst, cores))
+    return sum(len(topo.engines(k, dst)) for k in _relays(topo, src, dst, cores))
 
 
 def relay_program(g, core, T, topo):
@@ -84,8 +80,8 @@ def relay_program(g, core, T, topo):
         rid, pid = topo.addr(dst, core)
         sent = 0
         for s in range(1, H + 1):
-            g.wait_ge(T.sem["rl%d" % s], len(_first_hop(topo, src, dst, cores, s)[role][1]))
-            e = _second_hop(topo, core, dst, s)
+            g.wait_ge(T.sem["rl%d" % s], len(_first_hop(topo, src, dst, cores)[role][1]))
+            e = topo.engines(core, dst)
             if role == 0:
                 o, i = T["w%dc" % s][:, 256:320].bitcast(dt.uint8), T["r%dc" % s][:, 0:P].bitcast(dt.uint8)
             else:
@@ -119,18 +115,18 @@ def rank_program(g, core, T, topo):
     def qz(name, a, b, src):
         return V.quantize_mx(T[name + "c"][:, a:b], T[name + "s"][:, a:b], src)
 
-    def mm(out, l, la, r, ra, start=True, stop=True):
-        return E.matmul_mx(out[:, 0:128], T[l + "c"][:, la:la + 128], T[l + "s"][:, la:la + 128],
-                           T[r + "c"][:, ra:ra + 128], T[r + "s"][:, ra:ra + 128], start, stop)
+    def mm(out, l, la, r, ra, start=True, stop=True, k=128):
+        return E.matmul_mx(out[:, 0:k], T[l + "c"][:, la:la + 128], T[l + "s"][:, la:la + 128],
+                           T[r + "c"][:, ra:ra + k], T[r + "s"][:, ra:ra + k], start, stop)
 
     def send(s):
         name, a0 = SRC[s - 1]
-        (da, ea), (db, eb) = _first_hop(topo, core, nxt, cores, s)
+        (da, ea), (db, eb) = _first_hop(topo, core, nxt, cores)
         direct = da == nxt
         land, l0, sem = ("w%d" % s, 256, "arr%d" % s) if direct else ("r%d" % s, 0, "rl%d" % s)
         co, ci = T[land + "c"][:, l0:l0 + P].bitcast(dt.uint8), T[name + "c"][:, a0:a0 + P].bitcast(dt.uint8)
         (ra, pa), (rb, pb) = topo.addr(da, core), topo.addr(db, core)
-        if direct and s == 1:
+        if s == 1:
             g.remote_dma(co, ci, T.sem[sem], T.sem.sent, pa, ra, _mask(ea))
             g.remote_dma(T[land + "s"][:, l0:l0 + P], T[name + "s"][:, a0:a0 + P], T.sem[sem], T.sem.sent, pb, rb, _mask(eb))
         else:
@@ -141,122 +137,143 @@ def rank_program(g, core, T, topo):
             ], local_sem=T.sem.sent)
         cnt["sent"] = cnt.get("sent", 0) + len(ea) + len(eb)
 
-    cb = T.cb
+    cb, tt, qt, x1, x2 = T.cb, T.tt, T.qt, T.x1, T.x2
+    small = {"allow_small_or_imprecise_dtypes": True}
     sig(Y.dma_start(cb[:, PN0:PN0 + 256], T.pn[:]), "lpn", 16)
     sig(Y.dma_start(T.xt[:], T.x[:]), "lx", 16)
     sig(Y.dma_start(T.ut[:, 0:4], T.u[:]), "lu", 16)
     sig(Y.dma_start(T.wt[:], T.w[:]), "lw", 16)
-    sig(g.iota(T.di[:], [[1, 128]], 0, -1, allow_small_or_imprecise_dtypes=True), "g1")
-    sig(g.iota(T.d16[:], [[0, 8], [1, 16]], 0, -1, allow_small_or_imprecise_dtypes=True), "g2")
+    sig(g.iota(T.di[:], [[1, 128]], 0, -1, **small), "g1")
+    sig(g.iota(T.d16[:], [[0, 8], [1, 16]], 0, -1, **small), "g2")
     sig(g.iota(T.pi[:, 0:1], [[0, 1]], 0, 1), "g2")
     sig(V.memset(cb[:, FP0:FM0], 0.0), "a1")
-    sig(V.memset(T.tt[:], 0.0), "a2")
+    sig(V.memset(tt[:], 0.0), "a2")
     w(V, "g1", "a1")
     sig(V.tensor_scalar(cb[:, FP0 + 3:FP0 + 515:4], T.di[:], 0.0, None, A.is_equal), "a3")
-    sig(V.memset(cb[:, X10:WM0], 0.0), "a2")
-    w(V, "a3")
-    sig(qz("k0", 128, 256, cb[:, FP0 + 3:FP0 + 515]), "a4")
-    w(V, "lpn")
+    w(V, "a3", "lpn")
     sig(qz("k0", 0, 128, cb[:, PN0:PN0 + 512]), "qpn")
-    w(g, "a4", "qpn")
+    w(g, "qpn")
     send(1)
-    sig(g.iota(T.iot[:], [[1, 64]], 64, 0, allow_small_or_imprecise_dtypes=True), "g3")
-    sig(g.iota(T.inv[:], [[0, 3], [1, 192]], 128, 0, allow_small_or_imprecise_dtypes=True), "g4")
+    sig(g.iota(T.dm[:], [[0, 2], [1, 64]], 64, -1, **small), "g3")
+    sig(g.iota(T.iot[:], [[1, 64]], 64, 0, **small), "g3")
+    sig(g.iota(T.inv[:], [[0, 3], [1, 192]], 128, 0, **small), "g4")
+    w(S, "a3")
+    sig(S.activation(cb[:, FM0:Z0], cb[:, FP0:FM0], ACT.Copy, scale=-0.5), "s2")
     w(S, "g1", "lu")
     for t in range(4):
         sig(S.activation(T.ur[:, t:512:4], T.di[:], ACT.Identity, bias=T.ut[:, t:t + 1], scale=0.0), "s1")
-    w(S, "a3")
-    sig(S.activation(cb[:, FM0:Z0], cb[:, FP0:FM0], ACT.Copy, scale=-0.5), "s2")
+    sig(V.memset(x2[:], 0.0), "a2")
+    sig(V.memset(qt[:], 0.0), "a2")
+    w(V, "g2")
+    sig(V.tensor_scalar(T.pj[:, 0:1], T.pi[:, 0:1], 15, None, A.bitwise_and), "b0")
+    sig(V.tensor_scalar(T.pj[:, 1:2], T.pi[:, 0:1], 112, None, A.bitwise_and), "b0")
     w(V, "lx")
     sig(qz("w1", 128, 256, T.xt[:]), "qx")
-    w(V, "a2", "g2")
-    d = T.di[64:128, 64:128]
-    sig(V.tensor_scalar(T.tmp[64:128, 0:64], d, 0.0, None, A.is_gt), "b1")
-    sig(V.tensor_scalar(T.tmp[64:128, 64:128], d, 0.0, None, A.is_equal), "b1")
-    sig(V.tensor_scalar(T.pj[:, 0:1], T.pi[:, 0:1], 15, None, A.bitwise_and), "b1")
-    sig(V.tensor_scalar(T.pj[:, 1:2], T.pi[:, 0:1], 112, None, A.bitwise_and), "b1")
-    sig(V.tensor_scalar(cb[64:128, X10 + 4:WC0:8], d, 0.0, None, A.is_equal), "b2")
-    sig(V.memset(cb[0:1, X10:WC0:8], 1.0), "b2")
-    sig(V.memset(T.tt[0:1, 0:512:4], 1.0), "b2")
-    sig(V.memset(T.hh[:, 1:128:2], 0.5), "b2")
+    w(V, "b0", "a2")
+    sig(V.tensor_copy(T.pf[:, 0:2], T.pj[:, 0:2]), "b0")
+    sig(V.tensor_scalar(T.pf[:, 3:4], T.pj[:, 1:2], -1.0, None, A.mult), "b0")
+    for b in range(4):
+        sig(qz(EB[b][0], EB[b][1], EB[b][1] + 128, cb[:, FP0 + 3 - b:FP0 + 515 - b]), "qe")
+    w(V, "b0")
+    sig(V.tensor_scalar(T.mt[:], T.d16[:], T.pf[:, 3:4], None, A.is_equal), "b1")
+    sig(V.tensor_scalar(T.l3[:], T.d16[:], T.pf[:, 3:4], None, A.is_gt), "b1")
+    sig(V.tensor_scalar(T.l4[:], T.d16[:], T.pf[:, 3:4], -128.0, A.is_equal, A.mult), "b1")
+    sig(V.memset(tt[64:128, 3:512:4], 1.0), "b2")
+    sig(V.memset(tt[64:128, 1:2], 1.0), "b2")
+    sig(V.memset(qt[0:1, 0:512:4], 1.0), "b2")
+    sig(V.memset(qt[0:1, 3:512:4], 1.0), "b2")
+    w(V, "s2")
+    for b in range(4):
+        sig(qz(FB[b][0], FB[b][1], FB[b][1] + 128, cb[:, FM0 + 3 - b:FM0 + 515 - b]), "qe")
     w(V, "s1")
     sig(qz("uq", 0, 128, T.ur[:]), "qu")
-    w(V, "b1")
-    sig(V.tensor_tensor(cb[64:128, X10:WC0:8], T.tmp[64:128, 0:64], T.tmp[64:128, 64:128], A.subtract), "b2")
-    sig(V.tensor_tensor(cb[64:128, X10 + 1:WC0:8], T.tmp[64:128, 64:128], T.tmp[64:128, 0:64], A.subtract), "b2")
-    sig(V.tensor_copy(T.pf[:, 0:1], T.pj[:, 0:1]), "b2")
-    sig(V.tensor_scalar(T.pf[:, 1:2], T.pj[:, 1:2], -1.0, None, A.mult), "b2")
-    sig(V.memset(cb[:, WC0:WM0:4], 256.0), "b2")
-    sig(V.memset(cb[:, WM0:CBW:4], -256.0), "b2")
-    sig(V.memset(cb[:, WM0 + 2:CBW:4], 1.0), "b2")
-    sig(V.memset(cb[:, WM0 + 3:CBW:4], 0.0), "b2")
-    sig(V.tensor_scalar(cb[:, WM0 + 1:CBW:4], T.d16[:], 0.0, 512.0, A.is_equal, A.mult), "b2")
-    sig(V.tensor_scalar(cb[:, Q0 + 1:X10:4], T.d16[:, 0:64], 0.0, None, A.not_equal), "b2")
-    sig(V.memset(cb[:, Q0 + 3:X10:4], 0.0), "b2")
-    sig(V.memset(T.dp[:], -1000.0), "b2")
-    w(V, "b2")
-    sig(qz("k1", 0, 128, cb[:, X10:WC0]), "b3")
-    sig(qz("k1", 192, 448, cb[:, WC0:CBW]), "b3")
-    sig(V.tensor_scalar(T.dt1[:], T.d16[:], T.pf[:, 1:2], -1048576.0, A.is_equal, A.mult), "b4")
-    sig(V.tensor_scalar(T.pf[:, 2:3], T.pf[:, 0:1], -1024.0, 15360.0, A.mult, A.add), "b4")
     w(V, "g3")
-    sig(V.tensor_scalar(T.dp[:, 0:64:16], T.iot[:, 0:64:16], T.pf[:, 0:1], -192.0, A.add, A.add), "b4")
-    EB = [("k0", 128), ("k2", 0), ("k2", 192), ("k2", 320)]
-    for b in range(1, 4):
-        sig(qz(EB[b][0], EB[b][1], EB[b][1] + 128, cb[:, FP0 + 3 - b:FP0 + 515 - b]), "qe")
-    w(V, "s2", "lw")
-    for b in range(4):
-        sig(qz("k3", 128 * b, 128 * b + 128, cb[:, FM0 + 3 - b:FM0 + 515 - b]), "qe")
+    sig(V.tensor_scalar(x1[:, 2:512:4], T.dm[:], 0.0, None, A.is_equal), "b1")
+    sig(V.tensor_scalar(T.lt[:], T.dm[:], 0.0, None, A.is_gt), "b1")
+    sig(V.tensor_scalar(T.l2[:], T.dm[:], 0.0, -2.0, A.is_equal, A.mult), "b1")
+    kk = T.iot[:, 0:64:16]
+    sig(V.tensor_scalar(x2[:, 4:52:12], kk, T.pf[:, 1:2], None, A.is_equal), "b2")
+    sig(V.tensor_scalar(x2[:, 5:53:12], kk, T.pf[:, 1:2], 16.0, A.is_equal, A.mult), "b2")
+    sig(V.tensor_scalar(x2[64:128, 10:58:12], T.iot[64:128, 0:64:16], T.pf[64:128, 1:2], 256.0, A.is_equal, A.mult), "b2")
+    sig(V.tensor_scalar(x2[0:64, 10:58:12], T.di[0:64, 0:64:16], 0.0, 256.0, A.is_gt, A.mult), "b2")
+    sig(V.memset(x2[0:1, 8:56:12], 256.0), "b2")
+    sig(V.memset(x2[0:1, 11:59:12], 256.0 * (128 - G)), "b2")
+    w(V, "b1")
+    sig(V.tensor_tensor(x1[:, 0:512:4], x1[:, 2:512:4], T.lt[:], A.subtract), "b2")
+    sig(V.tensor_tensor(x1[:, 1:512:4], x1[:, 2:512:4], T.lt[:], A.subtract), "b2")
+    sig(V.tensor_tensor(x1[:, 3:512:4], T.l2[:], T.lt[:], A.add), "b2")
+    sig(V.tensor_tensor(T.ct[64:128, :], T.l3[64:128, :], T.l4[64:128, :], A.add), "b4")
+    sig(V.memset(T.ct[0:64, :], 1.0), "b4")
+    w(V, "b2")
+    sig(qz("k1", 0, 128, x1[:]), "b3")
+    sig(qz("k1", 192, 320, x2[:]), "b3")
+    sig(V.memset(T.dp[:, 0:12:3], -1e6), "b4")
+    sig(V.memset(T.dp[:, 1:12:3], 1e6), "b4")
+    sig(V.tensor_scalar(T.dp[:, 2:12:3], kk, T.pf[:, 0:1], 64.0, A.add, A.add), "b4")
+    sig(V.tensor_scalar(T.pf[:, 2:3], T.pf[:, 0:1], -1024.0, 15360.0, A.mult, A.add), "b4")
+    sig(V.tensor_scalar(T.dt2[:], T.mt[:], -1048576.0, 1024.0, A.mult, A.add), "b4")
+    w(V, "lw")
     sig(qz("wq", 0, 128, T.wt[:]), "qe")
-    w(V, "b4")
-    sig(V.tensor_scalar(T.dt2[:], T.dt1[:], 1024.0, None, A.add), "qe")
-    w(V, "qe", "g4")
-    zero = cb[:, WC0 + 1:WM0:4]
+    w(V, "qe", "g4", "b4")
+    w(S, "b1")
     w(E, "qx", "qu")
+    up = slice(64, 128)
 
     for h in range(1, H + 1):
         Wn, Wx = "w%d" % h, "w%d" % (h + 1)
         an, a0 = SRC[h]
         op, ot = T.offp[:, 4 * h:4 * h + 4], T.offt[:, 8 * h:8 * h + 8]
         iv = 192 * (h - 1)
-        sig(mm(T.pd, Wn, 128, "uq", 0), "tu")
-        w(S, "tu")
-        sig(S.activation(T.up[:, 0:1], T.pd[:, 0:1], ACT.Copy), "su")
-        E.wait_ge(T.sem["arr%d" % h], _arrival(topo, prv, core, cores, h))
-        sig(mm(T.pa, Wn, 192, Wn, 128), "ts")
-        sig(mm(T.pb, "uq", 0, Wn, 192), "tr")
-        w(S, "su", "tr")
-        sig(S.activation(T.hh[:, 0:128:2], T.pb[:, 64:128], ACT.Sign, bias=T.up[:, 0:1], scale=-1.0), "sh")
-        w(V, "ts")
-        sig(V.tensor_tensor_scan(T.pmx[64:128, :], T.pa[64:128, 0:128], cb[64:128, WC0 + 1:WM0:4], -1e29, A.max, A.add), "vs")
-        w(V, "vs")
-        sig(V.tensor_scalar(T.tt[64:128, 0:512:4], T.pmx[64:128, 0:128], T.pmx[64:128, 127:128], None, A.is_ge), "vt")
-        sig(V.tensor_scalar(T.tt[64:128, 5:512:4], T.pmx[64:128, 0:127], T.pmx[64:128, 127:128], None, A.is_ge), "vt")
-        w(V, "vt")
-        sig(qz("tq", 0, 128, T.tt[:]), "vq1")
-        if h == 1:
-            w(E, "b3")
-        w(E, "vq1")
-        sig(mm(T.pcc, "tq", 0, "k1", 0), "tv")
-        w(V, "tv", "sh")
-        sig(V.tensor_tensor(cb[:, Q0:X10:2], T.pcc[:, 0:128], T.hh[:], A.is_lt), "vq")
-        w(V, "vq")
-        sig(qz("qq", 0, 128, cb[:, Q0:Q0 + 512]), "vq2")
-        w(E, "vq2")
-        sig(mm(T.pcc, "k1", 192, "qq", 0), "tc")
-        sig(mm(T.pb, "k1", 320, "qq", 0), "tm")
-        if h == 1:
-            w(E, "a4", "qe")
-        for b in range(4):
+
+        def ousted(b, Wn=Wn):
             mm(T["pz%d" % b], EB[b][0], EB[b][1], Wn, 192, True, False)
-        w(V, "tc")
-        sig(V.tensor_tensor_scan(T.cc[:], T.pcc[:, 0:64], cb[:, WC0 + 1:WC0 + 256:4], -256.0 * (G + 1), A.add, A.add), "vc")
-        w(V, "vc", "tm")
-        sig(V.tensor_tensor(T.mm[:], T.pb[:, 0:64], T.cc[:], A.max), "vm")
-        w(V, "vm")
-        sig(V.tensor_tensor_scan(T.st[:], T.dp[:], T.mm[:], -1000.0, A.max, A.min), "vg")
+
+        sig(mm(T.pd, "uq", 0, Wn, 128), "tu")
+        w(S, "tu")
+        sig(S.activation(T.upr[up, :], T.pd[up, 0:128], ACT.Copy), "su")
+        E.wait_ge(T.sem["arr%d" % h], _arrival(topo, prv, core, cores))
+        sig(mm(T.pa, Wn, 192, Wn, 128), "ts")
+        sig(mm(T.pb, Wn, 192, "uq", 0), "tr")
+        if h == 1:
+            w(E, "qe", "b3")
+        ousted(0)
+        ousted(1)
+        if h == H:
+            w(Y, "sy", "ts")
+            sig(Y.dma_start(T.y[:, 0:P * (H - 1)], T.yy[:, 0:P * (H - 1)]), "st1", 16)
+        top = T.pmx[up, 127:128]
+        w(V, "ts")
+        sig(V.tensor_tensor_scan(T.pmx[up, :], T.pa[up, 0:128], x2[up, 256:384], -1e29, A.max, A.add), "vs")
+        w(V, "su", "tr")
+        sig(V.tensor_scalar(tt[up, 2:512:4], T.upr[up, :], T.pb[up, 0:1], None, A.is_gt), "vt")
+        w(V, "vs")
+        sig(V.tensor_scalar(tt[up, 0:512:4], T.pmx[up, :], top, None, A.is_ge), "vt")
+        w(S, "vs")
+        sig(S.activation(tt[up, 5:512:4], T.pmx[up, 0:127], ACT.Sign, bias=top, scale=-1.0, accum_out=T.nm[up, 0:1]), "sh")
+        sig(S.activation(T.tmp[up, :], T.pmx[up, 15:128:16], ACT.Sign, bias=top, scale=-1.0, accum_out=T.nm[up, 1:2]), "shi")
+        w(V, "vt", "sh")
+        sig(qz("tq", 0, 130, tt[:]), "vq1")
+        w(E, "vq1")
+        sig(mm(T.pcc, "k1", 0, "tq", 0, k=130), "tv")
+        ousted(2)
+        w(S, "sh", "shi")
+        sig(S.activation(T.nm[up, 2:3], T.nm[up, 1:2], ACT.Identity, bias=T.nm[up, 0:1], scale=-16.0), "slo")
+        sig(S.activation(qt[up, 1:512:4], T.mt[up, :], ACT.Identity, scale=T.nm[up, 1:2]), "sm")
+        w(S, "slo")
+        sig(S.activation(qt[up, 0:512:4], T.mt[up, :], ACT.Identity, scale=T.nm[up, 2:3]), "sm")
+        w(V, "tv")
+        sig(V.tensor_reduce(T.qf[:, 0:1], T.pcc[:, 0:130], AxisListType.X, A.max), "vr")
+        w(V, "vr")
+        sig(V.tensor_scalar(qt[:, 2:512:4], T.ct[:], T.qf[:, 0:1], None, A.mult), "vq")
+        w(V, "vq", "sm")
+        sig(qz("qq", 0, 128, qt[:]), "vq2")
+        w(E, "vq2")
+        sig(mm(T.pb, "qq", 0, "k1", 192), "tm")
+        ousted(3)
+        w(V, "tm")
+        sig(V.tensor_tensor_scan(T.st[:], T.pb[:, 0:12], T.dp[:], 0.0, A.max, A.min), "vg")
         w(V, "vg")
-        sig(V.tensor_scalar(op, T.st[:, 15:64:16], 256.0, None, A.add), "vo")
+        sig(V.tensor_copy(op, T.st[:, 2:12:3]), "vo")
         w(V, "vo")
         w(S, "vo")
         sig(V.tensor_copy(T[an + "c"][:, a0:a0 + P].bitcast(dt.uint32), T[Wn + "c"][:, 128:320].bitcast(dt.uint32).indirect(op)), "va")
@@ -267,21 +284,18 @@ def rank_program(g, core, T, topo):
         sig(V.tensor_copy(T.inv[:, iv:iv + 192].indirect(op), T.iot[:]), "vi")
         w(E, "va", "sa")
         for b in range(4):
-            sig(mm(T["pz%d" % b], "k3", 128 * b, an, a0 - 64, False, True), "tz%d" % b)
+            sig(mm(T["pz%d" % b], FB[b][0], FB[b][1], an, a0 - 64, False, True), "tz%d" % b)
         sig(mm(T.pd, "wq", 0, an, a0 - 64), "ty")
         w(V, "vi")
         sig(V.tensor_tensor_scan(T.stt[:], T.dt2[:], T.inv[:, iv:iv + 128], 0.0, A.add, A.max), "vst")
         w(V, "vst")
         sig(V.tensor_scalar(ot, T.stt[:, 15:128:16], T.pf[:, 2:3], None, A.subtract), "vot")
-        for b in (0, 2):
+        for b in range(4):
             w(S, "tz%d" % b)
             sig(S.activation(cb[:, Z0 + b:Q0:4], T["pz%d" % b][:, 64:128], ACT.Copy), "sz")
-        for b in (1, 3):
-            w(V, "tz%d" % b)
-            sig(V.tensor_copy(cb[:, Z0 + b:Q0:4], T["pz%d" % b][:, 64:128]), "vz")
         w(S, "ty")
         sig(S.activation(T.yy[:, P * (h - 1):P * h], T.pd[:, 64:128], ACT.Copy), "sy")
-        w(V, "vz", "sz")
+        w(V, "sz")
         sig(qz(Wn, 0, 128, cb[:, Z0 - 256:Q0]), "vqz")
         w(V, "vqz", "vot")
         w(S, "vqz", "vot")
@@ -297,12 +311,13 @@ def rank_program(g, core, T, topo):
     for k in range(4):
         sig(Y.dma_start(T.psc[4 * k:4 * k + 4, :], T[an + "s"][32 * k:32 * k + 4, a0:a0 + P]), "st1", 16)
     w(Y, "sy")
-    sig(Y.dma_start(T.y[:], T.yy[:]), "st1", 16)
+    sig(Y.dma_start(T.y[:, P * (H - 1):P * H], T.yy[:, P * (H - 1):P * H]), "st1", 16)
     w(Y, "vb")
     sig(Y.dma_start(T.oc[:], T.w4c[:, 128:256].bitcast(dt.uint8)), "st1", 16)
+    w(Y, "sb")
     w(S, "sb")
     for k in range(4):
-        sig(S.dma_start(T.osc[4 * k:4 * k + 4, :], T.w4s[32 * k:32 * k + 4, 128:256]), "st2", 16)
+        sig((Y if k == 3 else S).dma_start(T.osc[4 * k:4 * k + 4, :], T.w4s[32 * k:32 * k + 4, 128:256]), "st1" if k == 3 else "st2", 16)
     w(Y, "st1")
     w(S, "st2")
     for nm in cnt:

@@ -3,24 +3,25 @@ from concourse.mybir import dt, AluOpType, AxisListType, ActivationFunctionType
 
 P, C, G, H = 64, 128, 16, 3
 X4, U8, BF, F32 = "float8_e4m3fn_x4", "uint8", "bfloat16", "float32"
-PN0, FP0, FM0, Z0, Q0 = 0, 256, 776, 1296, 1552
+FP0, FM0, ZP, Z0, Q0 = 0, 520, 784, 1040, 1296
 SRC = [("k0", 0), ("k1", 128), ("k2", 128), ("k3", 512)]
 EB = [("k0", 128), ("k2", 0), ("k2", 192), ("k1", 320)]
 FB = [("k2", 320), ("k3", 128), ("k3", 256), ("k3", 384)]
 PAD = 256
+NT = C + 4
+ST = 13
+QW = ST * C - 8
 
 SCRATCH = {
-    "cb": ("sbuf", [128, Q0], BF), "xt": ("sbuf", [128, 512], BF), "wt": ("sbuf", [128, 512], BF),
-    "ut": ("sbuf", [128, 8], BF), "ur": ("sbuf", [128, 512], BF), "tt": ("sbuf", [128, 520], BF),
-    "x1": ("sbuf", [128, 512], BF), "x2": ("sbuf", [128, 512], BF), "qt": ("sbuf", [128, 512], BF),
-    "ct": ("sbuf", [128, 128], BF), "mt": ("sbuf", [128, 128], BF), "lt": ("sbuf", [128, 128], BF),
-    "l2": ("sbuf", [128, 128], BF), "l3": ("sbuf", [128, 128], BF), "l4": ("sbuf", [128, 128], BF),
-    "di": ("sbuf", [128, 128], F32), "d16": ("sbuf", [128, 128], F32), "dm": ("sbuf", [128, 128], F32),
-    "pi": ("sbuf", [128, 4], "int32"),
+    "cb": ("sbuf", [128, Q0], BF), "pt": ("sbuf", [128, 512], BF), "xt": ("sbuf", [128, 512], BF),
+    "wt": ("sbuf", [128, 512], BF), "ut": ("sbuf", [128, 8], BF), "ur": ("sbuf", [128, 1024], BF),
+    "tt": ("sbuf", [128, 4 * NT], BF), "x1": ("sbuf", [128, 512], BF), "x2": ("sbuf", [128, 512], BF),
+    "qt": ("sbuf", [128, QW + 512], BF), "mt": ("sbuf", [128, 128], BF), "zz": ("sbuf", [128, 136], BF),
+    "di": ("sbuf", [128, 128], F32), "d16": ("sbuf", [128, 128], F32), "rc": ("sbuf", [128, 128], F32),
+    "pi": ("sbuf", [128, 4], "int32"), "mk": ("sbuf", [128, 4], F32),
     "pj": ("sbuf", [128, 4], "int32"), "pf": ("sbuf", [128, 4], F32), "iot": ("sbuf", [128, 64], F32),
     "inv": ("sbuf", [128, 576], F32), "tmp": ("sbuf", [128, 8], F32), "dp": ("sbuf", [128, 12], F32),
-    "dt2": ("sbuf", [128, 128], F32), "upr": ("sbuf", [128, 128], F32),
-    "nm": ("sbuf", [128, 4], F32), "qf": ("sbuf", [128, 4], F32), "pmx": ("sbuf", [128, 128], F32),
+    "dt2": ("sbuf", [128, 128], F32), "nm": ("sbuf", [128, 4], F32), "pmx": ("sbuf", [128, 128], F32),
     "st": ("sbuf", [128, 12], F32), "stt": ("sbuf", [128, 128], F32),
     "offp": ("sbuf", [128, 16], "uint16"), "offt": ("sbuf", [128, 32], "uint16"), "yy": ("sbuf", [128, 192], F32),
     "pa": ("psum", [128, 512], F32), "pb": ("psum", [128, 512], F32), "pcc": ("psum", [128, 512], F32),
@@ -29,16 +30,16 @@ SCRATCH = {
 for _b in range(4):
     SCRATCH["pz%d" % _b] = ("psum", [128, 512], F32)
 for _n, _w, _ws in (("k0", 256, 256), ("k1", 448, 448), ("k2", 448, 448), ("k3", 576, 576), ("wq", 128, 128),
-                    ("uq", 128, 128), ("tq", 132, 132), ("qq", 128, 128), ("w1", 320, 512), ("w2", 320, 512),
+                    ("uq", 256, 256), ("tq", NT, NT), ("qq", 128, 128), ("w1", 320, 512), ("w2", 320, 512),
                     ("w3", 320, 512), ("w4", 256, 256), ("r1", 64, PAD), ("r2", 64, PAD), ("r3", 64, PAD)):
     SCRATCH[_n + "c"] = ("sbuf", [128, _w], X4)
     SCRATCH[_n + "s"] = ("sbuf", [128, _ws], U8)
 
-SEMAPHORES = ["lpn", "lx", "lu", "lw", "g1", "g2", "g3", "g4", "a1", "a2", "a3", "qpn", "qx", "qu", "b0", "b1", "b2",
-              "b3", "b4", "qe", "s1", "s2", "arr1", "arr2", "arr3", "rl1", "rl2", "rl3", "sent",
-              "tu", "ts", "tr", "tv", "tm", "tz0", "tz1", "tz2", "tz3", "ty",
-              "vs", "vt", "vq1", "vr", "vq", "vq2", "vg", "vo", "va", "vi", "vst", "vot", "vqz", "vb",
-              "su", "sh", "shi", "slo", "sm", "sa", "sz", "sy", "sb", "st1", "st2"]
+SEMAPHORES = ["lpn", "lx", "lu", "lw", "g1", "g2", "g3", "g4", "g5", "g6", "a1", "a2", "a3", "qpn", "qx", "qu", "b0", "b1",
+              "b2", "b3", "b4", "b5", "qe", "s1", "s2", "s3", "s4", "s5", "arr1", "arr2", "arr3", "rl1", "rl2", "rl3", "sent",
+              "ts", "td", "tv", "tm", "tz0", "tz1", "tz2", "tz3", "ty",
+              "vs", "vt", "vq1", "vr", "vq2", "vg", "vo", "va", "vi", "vst", "vot", "vqz", "vb",
+              "sf", "sh", "shi", "slo", "sm", "sa", "sz", "sy", "sb", "st1", "st2"]
 
 
 def _mask(engines):
@@ -137,87 +138,93 @@ def rank_program(g, core, T, topo):
             ], local_sem=T.sem.sent)
         cnt["sent"] = cnt.get("sent", 0) + len(ea) + len(eb)
 
-    cb, tt, qt, x1, x2 = T.cb, T.tt, T.qt, T.x1, T.x2
+    cb, tt, qt, x1, x2, zz = T.cb, T.tt, T.qt, T.x1, T.x2, T.zz
     small = {"allow_small_or_imprecise_dtypes": True}
-    sig(Y.dma_start(cb[:, PN0:PN0 + 256], T.pn[:]), "lpn", 16)
+    low, up = slice(0, 64), slice(64, 128)
+
+    def places(h):
+        sig(g.iota(T.inv[:, 192 * (h - 1):192 * (h - 1) + C], [[1, C]], C, 0, **small), "g6")
+
+    sig(Y.dma_start(T.pt[:, 0:256], T.pn[:]), "lpn", 16)
     sig(Y.dma_start(T.xt[:], T.x[:]), "lx", 16)
     sig(Y.dma_start(T.ut[:, 0:4], T.u[:]), "lu", 16)
     sig(Y.dma_start(T.wt[:], T.w[:]), "lw", 16)
     sig(g.iota(T.di[:], [[1, 128]], 0, -1, **small), "g1")
-    sig(g.iota(T.d16[:], [[0, 8], [1, 16]], 0, -1, **small), "g2")
     sig(g.iota(T.pi[:, 0:1], [[0, 1]], 0, 1), "g2")
-    sig(V.memset(cb[:, FP0:FM0], 0.0), "a1")
+    sig(g.iota(T.iot[:], [[1, 64]], 64, 0, **small), "g3")
+    sig(V.memset(T.pt[:, 256:512], 0.0), "a1")
+    sig(V.memset(x2[:], 256.0), "a2")
     sig(V.memset(tt[:], 0.0), "a2")
-    w(V, "g1", "a1")
-    sig(V.tensor_scalar(cb[:, FP0 + 3:FP0 + 515:4], T.di[:], 0.0, None, A.is_equal), "a3")
-    w(V, "a3", "lpn")
-    sig(qz("k0", 0, 128, cb[:, PN0:PN0 + 512]), "qpn")
+    sig(V.memset(cb[:, FP0:FM0], 0.0), "a2")
+    sig(V.memset(zz[:], 0.0), "a2")
+    w(V, "g1")
+    sig(V.tensor_scalar(T.rc[:], T.di[:], -65.0, -63.0, A.max, A.min), "a3")
+    w(V, "a1", "lpn")
+    sig(qz("k0", 0, 128, T.pt[:]), "qpn")
     w(g, "qpn")
     send(1)
-    sig(g.iota(T.dm[:], [[0, 2], [1, 64]], 64, -1, **small), "g3")
-    sig(g.iota(T.iot[:], [[1, 64]], 64, 0, **small), "g3")
-    sig(g.iota(T.inv[:], [[0, 3], [1, 192]], 128, 0, **small), "g4")
+    sig(g.iota(T.d16[:], [[0, 8], [1, 16]], 0, -1, **small), "g4")
+    w(g, "a2")
+    pat = [[0, 8], [1, 16], [16, 4]]
+    sig(g.affine_select(x2[low, :], x2[low, :], pat, A.is_ge, 0.0, 0, -1), "g5")
+    w(g, "g5")
+    sig(g.affine_select(x2[low, :], x2[low, :], pat, A.not_equal, -256.0 * P, 0, -1), "g5")
+    places(1)
     w(S, "a3")
-    sig(S.activation(cb[:, FM0:Z0], cb[:, FP0:FM0], ACT.Copy, scale=-0.5), "s2")
-    w(S, "g1", "lu")
+    sig(S.activation(x1[:, 3:512:4], T.rc[:], ACT.Abs, bias=128.5, scale=2.0), "s3")
+    w(S, "lu")
     for t in range(4):
         sig(S.activation(T.ur[:, t:512:4], T.di[:], ACT.Identity, bias=T.ut[:, t:t + 1], scale=0.0), "s1")
-    sig(V.memset(x2[:], 0.0), "a2")
-    sig(V.memset(qt[:], 0.0), "a2")
-    w(V, "g2")
+    w(S, "s3")
+    for t, f in ((0, ACT.Identity), (1, ACT.Identity), (2, ACT.Relu)):
+        sig(S.activation(x1[:, t:512:4], x1[:, 3:512:4], f, bias=1.5, scale=-1.0), "s4")
+    w(S, "s1")
+    sig(S.activation(T.ur[:, 512:1024], T.ur[:, 0:512], ACT.Copy, scale=-1.0), "s1")
+    sig(V.memset(qt[:, QW:QW + 512], 0.0), "b2")
+    w(V, "g2", "a2")
     sig(V.tensor_scalar(T.pj[:, 0:1], T.pi[:, 0:1], 15, None, A.bitwise_and), "b0")
     sig(V.tensor_scalar(T.pj[:, 1:2], T.pi[:, 0:1], 112, None, A.bitwise_and), "b0")
+    sig(V.tensor_scalar(cb[:, FP0 + 3:FP0 + 515:4], T.di[:], 0.0, None, A.is_equal), "b5")
+    w(S, "b5")
+    sig(S.activation(cb[:, FM0:Z0], cb[:, FP0:FM0], ACT.Copy, scale=-0.5), "s2")
     w(V, "lx")
     sig(qz("w1", 128, 256, T.xt[:]), "qx")
-    w(V, "b0", "a2")
+    w(V, "b0", "b2")
     sig(V.tensor_copy(T.pf[:, 0:2], T.pj[:, 0:2]), "b0")
     sig(V.tensor_scalar(T.pf[:, 3:4], T.pj[:, 1:2], -1.0, None, A.mult), "b0")
+    sig(V.memset(tt[up, 1:2], 1.0), "b2")
+    sig(V.memset(zz[:, C:C + 1], -1.0), "b2")
+    sig(V.memset(qt[64:65, QW + 10:QW + 58:12], float(P - G)), "b2")
+    sig(V.memset(qt[64:65, QW + 11:QW + 59:12], 1.0), "b2")
+    sig(V.memset(T.dp[:, 0:12:3], -1e6), "b2")
+    sig(V.memset(T.dp[:, 1:12:3], 1e6), "b2")
+    w(V, "s4")
+    sig(qz("k1", 0, 128, x1[:]), "b3")
+    w(V, "b5")
     for b in range(4):
         sig(qz(EB[b][0], EB[b][1], EB[b][1] + 128, cb[:, FP0 + 3 - b:FP0 + 515 - b]), "qe")
-    w(V, "b0")
+    w(V, "s1")
+    sig(qz("uq", 0, 256, T.ur[:]), "qu")
+    w(V, "b0", "g3", "g4")
     sig(V.tensor_scalar(T.mt[:], T.d16[:], T.pf[:, 3:4], None, A.is_equal), "b1")
-    sig(V.tensor_scalar(T.l3[:], T.d16[:], T.pf[:, 3:4], None, A.is_gt), "b1")
-    sig(V.tensor_scalar(T.l4[:], T.d16[:], T.pf[:, 3:4], -128.0, A.is_equal, A.mult), "b1")
-    sig(V.memset(tt[64:128, 3:512:4], 1.0), "b2")
-    sig(V.memset(tt[64:128, 1:2], 1.0), "b2")
-    sig(V.memset(qt[0:1, 0:512:4], 1.0), "b2")
-    sig(V.memset(qt[0:1, 3:512:4], 1.0), "b2")
+    w(S, "b1")
+    sig(S.activation(x2[up, 0:512:4], T.mt[up, :], ACT.Copy), "s5")
+    sig(S.activation(x2[up, 1:512:4], T.mt[up, :], ACT.Copy, scale=16.0), "s5")
+    kk = T.iot[:, 0:64:16]
+    sig(V.tensor_scalar(T.mk[:], kk, T.pf[:, 1:2], None, A.is_equal), "b4")
+    sig(V.tensor_scalar(T.dp[:, 2:12:3], kk, T.pf[:, 0:1], 64.0, A.add, A.add), "b4")
+    sig(V.tensor_scalar(T.pf[:, 2:3], T.pf[:, 0:1], -1024.0, 15360.0, A.mult, A.add), "b4")
     w(V, "s2")
     for b in range(4):
         sig(qz(FB[b][0], FB[b][1], FB[b][1] + 128, cb[:, FM0 + 3 - b:FM0 + 515 - b]), "qe")
-    w(V, "s1")
-    sig(qz("uq", 0, 128, T.ur[:]), "qu")
-    w(V, "g3")
-    sig(V.tensor_scalar(x1[:, 2:512:4], T.dm[:], 0.0, None, A.is_equal), "b1")
-    sig(V.tensor_scalar(T.lt[:], T.dm[:], 0.0, None, A.is_gt), "b1")
-    sig(V.tensor_scalar(T.l2[:], T.dm[:], 0.0, -2.0, A.is_equal, A.mult), "b1")
-    kk = T.iot[:, 0:64:16]
-    sig(V.tensor_scalar(x2[:, 4:52:12], kk, T.pf[:, 1:2], None, A.is_equal), "b2")
-    sig(V.tensor_scalar(x2[:, 5:53:12], kk, T.pf[:, 1:2], 16.0, A.is_equal, A.mult), "b2")
-    sig(V.tensor_scalar(x2[64:128, 10:58:12], T.iot[64:128, 0:64:16], T.pf[64:128, 1:2], 256.0, A.is_equal, A.mult), "b2")
-    sig(V.tensor_scalar(x2[0:64, 10:58:12], T.di[0:64, 0:64:16], 0.0, 256.0, A.is_gt, A.mult), "b2")
-    sig(V.memset(x2[0:1, 8:56:12], 256.0), "b2")
-    sig(V.memset(x2[0:1, 11:59:12], 256.0 * (128 - G)), "b2")
     w(V, "b1")
-    sig(V.tensor_tensor(x1[:, 0:512:4], x1[:, 2:512:4], T.lt[:], A.subtract), "b2")
-    sig(V.tensor_tensor(x1[:, 1:512:4], x1[:, 2:512:4], T.lt[:], A.subtract), "b2")
-    sig(V.tensor_tensor(x1[:, 3:512:4], T.l2[:], T.lt[:], A.add), "b2")
-    sig(V.tensor_tensor(T.ct[64:128, :], T.l3[64:128, :], T.l4[64:128, :], A.add), "b4")
-    sig(V.memset(T.ct[0:64, :], 1.0), "b4")
-    w(V, "b2")
-    sig(qz("k1", 0, 128, x1[:]), "b3")
-    sig(qz("k1", 192, 320, x2[:]), "b3")
-    sig(V.memset(T.dp[:, 0:12:3], -1e6), "b4")
-    sig(V.memset(T.dp[:, 1:12:3], 1e6), "b4")
-    sig(V.tensor_scalar(T.dp[:, 2:12:3], kk, T.pf[:, 0:1], 64.0, A.add, A.add), "b4")
-    sig(V.tensor_scalar(T.pf[:, 2:3], T.pf[:, 0:1], -1024.0, 15360.0, A.mult, A.add), "b4")
     sig(V.tensor_scalar(T.dt2[:], T.mt[:], -1048576.0, 1024.0, A.mult, A.add), "b4")
     w(V, "lw")
     sig(qz("wq", 0, 128, T.wt[:]), "qe")
-    w(V, "qe", "g4", "b4")
-    w(S, "b1")
+    w(V, "qe", "b2", "b3", "b4")
+    w(S, "b2", "b4")
     w(E, "qx", "qu")
-    up = slice(64, 128)
+    direct_in = topo.may_write(prv, core)
 
     for h in range(1, H + 1):
         Wn, Wx = "w%d" % h, "w%d" % (h + 1)
@@ -228,12 +235,14 @@ def rank_program(g, core, T, topo):
         def ousted(b, Wn=Wn):
             mm(T["pz%d" % b], EB[b][0], EB[b][1], Wn, 192, True, False)
 
-        sig(mm(T.pd, "uq", 0, Wn, 128), "tu")
-        w(S, "tu")
-        sig(S.activation(T.upr[up, :], T.pd[up, 0:128], ACT.Copy), "su")
+        late = h == (3 if direct_in else 2)
+        if not late:
+            mm(T.pb, "uq", 0, Wn, 128, True, False)
         E.wait_ge(T.sem["arr%d" % h], _arrival(topo, prv, core, cores))
         sig(mm(T.pa, Wn, 192, Wn, 128), "ts")
-        sig(mm(T.pb, Wn, 192, "uq", 0), "tr")
+        if late:
+            mm(T.pb, "uq", 0, Wn, 128, True, False)
+        sig(mm(T.pb, Wn, 192, "uq", 128, False, True), "td")
         if h == 1:
             w(E, "qe", "b3")
         ousted(0)
@@ -243,49 +252,54 @@ def rank_program(g, core, T, topo):
             sig(Y.dma_start(T.y[:, 0:P * (H - 1)], T.yy[:, 0:P * (H - 1)]), "st1", 16)
         top = T.pmx[up, 127:128]
         w(V, "ts")
-        sig(V.tensor_tensor_scan(T.pmx[up, :], T.pa[up, 0:128], x2[up, 256:384], -1e29, A.max, A.add), "vs")
-        w(V, "su", "tr")
-        sig(V.tensor_scalar(tt[up, 2:512:4], T.upr[up, :], T.pb[up, 0:1], None, A.is_gt), "vt")
+        sig(V.tensor_tensor_scan(T.pmx[up, :], T.pa[up, 0:128], zz[up, 0:C], -1e29, A.max, A.add), "vs")
         w(V, "vs")
-        sig(V.tensor_scalar(tt[up, 0:512:4], T.pmx[up, :], top, None, A.is_ge), "vt")
+        sig(V.tensor_scalar(tt[up, 0:512:4], T.pmx[up, :], top, 1.0, A.is_ge, A.subtract), "vt")
+        w(S, "td")
+        sig(S.activation(tt[up, 2:512:4], T.pb[up, 0:128], ACT.Sign), "sf")
         w(S, "vs")
         sig(S.activation(tt[up, 5:512:4], T.pmx[up, 0:127], ACT.Sign, bias=top, scale=-1.0, accum_out=T.nm[up, 0:1]), "sh")
         sig(S.activation(T.tmp[up, :], T.pmx[up, 15:128:16], ACT.Sign, bias=top, scale=-1.0, accum_out=T.nm[up, 1:2]), "shi")
-        w(V, "vt", "sh")
-        sig(qz("tq", 0, 130, tt[:]), "vq1")
+        w(V, "vt", "sf", "sh")
+        sig(qz("tq", 0, NT, tt[:]), "vq1")
+        if h == 1:
+            w(V, "g5", "s5")
+            sig(qz("k1", 192, 320, x2[:]), "b3")
         w(E, "vq1")
-        sig(mm(T.pcc, "k1", 0, "tq", 0, k=130), "tv")
+        sig(mm(T.pcc, "k1", 0, "tq", 0, k=NT), "tv")
         ousted(2)
         w(S, "sh", "shi")
         sig(S.activation(T.nm[up, 2:3], T.nm[up, 1:2], ACT.Identity, bias=T.nm[up, 0:1], scale=-16.0), "slo")
-        sig(S.activation(qt[up, 1:512:4], T.mt[up, :], ACT.Identity, scale=T.nm[up, 1:2]), "sm")
+        sig(S.activation(qt[up, QW + 5:QW + 53:12], T.mk[up, :], ACT.Identity, scale=T.nm[up, 1:2]), "sm")
         w(S, "slo")
-        sig(S.activation(qt[up, 0:512:4], T.mt[up, :], ACT.Identity, scale=T.nm[up, 2:3]), "sm")
+        sig(S.activation(qt[up, QW + 4:QW + 52:12], T.mk[up, :], ACT.Identity, scale=T.nm[up, 2:3]), "sm")
         w(V, "tv")
-        sig(V.tensor_reduce(T.qf[:, 0:1], T.pcc[:, 0:130], AxisListType.X, A.max), "vr")
-        w(V, "vr")
-        sig(V.tensor_scalar(qt[:, 2:512:4], T.ct[:], T.qf[:, 0:1], None, A.mult), "vq")
-        w(V, "vq", "sm")
-        sig(qz("qq", 0, 128, qt[:]), "vq2")
-        w(E, "vq2")
-        sig(mm(T.pb, "qq", 0, "k1", 192), "tm")
+        sig(V.tensor_tensor_scan(qt[low, 0:ST * NT:ST], T.pcc[low, 0:NT], zz[low, 0:NT], 1.0, A.max, A.add), "vr")
+        w(V, "vr", "sm")
+        sig(qz("qq", 0, 128, qt[:, QW:QW + 512]), "vq2")
+        w(E, "vq2", "b3")
+        sig(mm(T.pd, "k1", 192, "qq", 0), "tm")
         ousted(3)
         w(V, "tm")
-        sig(V.tensor_tensor_scan(T.st[:], T.pb[:, 0:12], T.dp[:], 0.0, A.max, A.min), "vg")
+        sig(V.tensor_tensor_scan(T.st[:], T.pd[:, 0:12], T.dp[:], 0.0, A.max, A.min), "vg")
         w(V, "vg")
         sig(V.tensor_copy(op, T.st[:, 2:12:3]), "vo")
         w(V, "vo")
         w(S, "vo")
         sig(V.tensor_copy(T[an + "c"][:, a0:a0 + P].bitcast(dt.uint32), T[Wn + "c"][:, 128:320].bitcast(dt.uint32).indirect(op)), "va")
         sig(S.activation(T[an + "s"][:, a0:a0 + P], T[Wn + "s"][:, 128:320].indirect(op), ACT.Copy), "sa")
+        w(V, "g6")
         if h < H:
             w(g, "va", "sa")
+            if h == 1:
+                w(g, "b3")
             send(h + 1)
+            places(h + 1)
         sig(V.tensor_copy(T.inv[:, iv:iv + 192].indirect(op), T.iot[:]), "vi")
         w(E, "va", "sa")
         for b in range(4):
             sig(mm(T["pz%d" % b], FB[b][0], FB[b][1], an, a0 - 64, False, True), "tz%d" % b)
-        sig(mm(T.pd, "wq", 0, an, a0 - 64), "ty")
+        sig(mm(T.pcc, "wq", 0, an, a0 - 64), "ty")
         w(V, "vi")
         sig(V.tensor_tensor_scan(T.stt[:], T.dt2[:], T.inv[:, iv:iv + 128], 0.0, A.add, A.max), "vst")
         w(V, "vst")
@@ -294,9 +308,9 @@ def rank_program(g, core, T, topo):
             w(S, "tz%d" % b)
             sig(S.activation(cb[:, Z0 + b:Q0:4], T["pz%d" % b][:, 64:128], ACT.Copy), "sz")
         w(S, "ty")
-        sig(S.activation(T.yy[:, P * (h - 1):P * h], T.pd[:, 64:128], ACT.Copy), "sy")
+        sig(S.activation(T.yy[:, P * (h - 1):P * h], T.pcc[:, 64:128], ACT.Copy), "sy")
         w(V, "sz")
-        sig(qz(Wn, 0, 128, cb[:, Z0 - 256:Q0]), "vqz")
+        sig(qz(Wn, 0, 128, cb[:, ZP:Q0]), "vqz")
         w(V, "vqz", "vot")
         w(S, "vqz", "vot")
         sig(V.tensor_copy(T[Wx + "c"][:, 128:256].bitcast(dt.uint32), T[Wn + "c"][:, 0:256].bitcast(dt.uint32).indirect(ot)), "vb")

@@ -4,10 +4,10 @@ from concourse.mybir import dt, AluOpType, AxisListType, ActivationFunctionType
 P, C, G, H = 64, 128, 16, 3
 X4, U8, BF, F32 = "float8_e4m3fn_x4", "uint8", "bfloat16", "float32"
 FP0, FM0, ZP, Z0, Q0 = 0, 520, 784, 1040, 1296
-SRC = [("k0", 0), ("k1", 128), ("k2", 128), ("k3", 512)]
+SRC = [("k0", 0), ("k1", 128), ("k2", 128), ("k3", 576)]
 EB = [("k0", 128), ("k2", 0), ("k2", 192), ("k1", 320)]
-FB = [("k2", 320), ("k3", 128), ("k3", 256), ("k3", 384)]
-PAD = 256
+FB = [("k2", 320), ("k3", 192), ("k3", 320), ("k3", 448)]
+E0 = 128
 NT = C + 4
 ST = 13
 QW = ST * C - 8
@@ -16,30 +16,30 @@ SCRATCH = {
     "cb": ("sbuf", [128, Q0], BF), "pt": ("sbuf", [128, 512], BF), "xt": ("sbuf", [128, 512], BF),
     "wt": ("sbuf", [128, 512], BF), "ut": ("sbuf", [128, 8], BF), "ur": ("sbuf", [128, 1024], BF),
     "tt": ("sbuf", [128, 4 * NT], BF), "x1": ("sbuf", [128, 512], BF), "x2": ("sbuf", [128, 512], BF),
+    "x3": ("sbuf", [128, 512], BF), "sp": ("sbuf", [128, 4 * NT], BF), "cs": ("sbuf", [128, 8], F32),
     "qt": ("sbuf", [128, QW + 512], BF), "mt": ("sbuf", [128, 128], BF), "zz": ("sbuf", [128, 136], BF),
     "di": ("sbuf", [128, 128], F32), "d16": ("sbuf", [128, 128], F32), "rc": ("sbuf", [128, 128], F32),
     "pi": ("sbuf", [128, 4], "int32"), "mk": ("sbuf", [128, 4], F32),
     "pj": ("sbuf", [128, 4], "int32"), "pf": ("sbuf", [128, 4], F32), "iot": ("sbuf", [128, 64], F32),
-    "inv": ("sbuf", [128, 576], F32), "tmp": ("sbuf", [128, 8], F32), "dp": ("sbuf", [128, 12], F32),
+    "inv": ("sbuf", [128, 576], F32), "tmp": ("sbuf", [128, 8], F32), "dp": ("sbuf", [128, 4], F32),
     "dt2": ("sbuf", [128, 128], F32), "nm": ("sbuf", [128, 4], F32), "pmx": ("sbuf", [128, 128], F32),
-    "st": ("sbuf", [128, 12], F32), "stt": ("sbuf", [128, 128], F32),
+    "stt": ("sbuf", [128, 128], F32),
     "offp": ("sbuf", [128, 16], "uint16"), "offt": ("sbuf", [128, 32], "uint16"), "yy": ("sbuf", [128, 192], F32),
     "pa": ("psum", [128, 512], F32), "pb": ("psum", [128, 512], F32), "pcc": ("psum", [128, 512], F32),
     "pd": ("psum", [128, 512], F32),
 }
 for _b in range(4):
     SCRATCH["pz%d" % _b] = ("psum", [128, 512], F32)
-for _n, _w, _ws in (("k0", 256, 256), ("k1", 448, 448), ("k2", 448, 448), ("k3", 576, 576), ("wq", 128, 128),
-                    ("uq", 256, 256), ("tq", NT, NT), ("qq", 128, 128), ("w1", 320, 512), ("w2", 320, 512),
-                    ("w3", 320, 512), ("w4", 256, 256), ("r1", 64, PAD), ("r2", 64, PAD), ("r3", 64, PAD)):
+for _n, _w in (("k0", 256), ("k1", 448), ("k2", 448), ("k3", 640), ("wq", 128), ("uq", 256), ("tq", NT), ("qq", 128),
+               ("sq", NT), ("w1", 320), ("w2", 320), ("w3", 320), ("w4", 256), ("r1", 64), ("r2", 64), ("r3", 64)):
     SCRATCH[_n + "c"] = ("sbuf", [128, _w], X4)
-    SCRATCH[_n + "s"] = ("sbuf", [128, _ws], U8)
+    SCRATCH[_n + "s"] = ("sbuf", [128, _w], U8)
 
-SEMAPHORES = ["lpn", "lx", "lu", "lw", "g1", "g2", "g3", "g4", "g5", "g6", "a1", "a2", "a3", "qpn", "qx", "qu", "b0", "b1",
-              "b2", "b3", "b4", "b5", "qe", "s1", "s2", "s3", "s4", "s5", "arr1", "arr2", "arr3", "rl1", "rl2", "rl3", "sent",
-              "ts", "td", "tv", "tm", "tz0", "tz1", "tz2", "tz3", "ty",
-              "vs", "vt", "vq1", "vr", "vq2", "vg", "vo", "va", "vi", "vst", "vot", "vqz", "vb",
-              "sf", "sh", "shi", "slo", "sm", "sa", "sz", "sy", "sb", "st1", "st2"]
+SEMAPHORES = ["lpn", "lx", "lu", "lw", "g1", "g2", "g3", "g4", "g5", "g6", "g7", "a1", "a2", "a3", "qpn", "qx", "qu", "b0",
+              "b1", "b2", "b3", "b4", "b5", "b6", "b7", "qe", "s1", "s2", "s3", "s4", "s5", "s6", "arr1", "arr2", "arr3",
+              "rl1", "rl2", "rl3", "sent", "ts", "td", "tv", "tm", "tn", "tz0", "tz1", "tz2", "tz3", "ty",
+              "vs", "c1", "vq1", "c2", "vq2", "vo", "va", "sa", "vi", "vst", "c4", "c5", "c6", "c7", "vsp", "vn", "vb",
+              "shi", "slo", "sz", "sy", "sb", "st1", "st2"]
 
 
 def _mask(engines):
@@ -51,18 +51,21 @@ def _mask(engines):
 
 def _relays(topo, src, dst, cores):
     c = [k for k in topo.cores_of(src) if k not in cores and topo.may_write(k, dst)]
-    c = [k for k in c if topo.die(k) == topo.die(src)] + [k for k in c if topo.die(k) != topo.die(src)]
-    return c[:2]
+    same = [k for k in c if topo.die(k) == topo.die(src)]
+    other = [k for k in c if topo.die(k) != topo.die(src)]
+    return [same[0], other[0]] if same and other else c[:2]
 
 
-def _first_hop(topo, src, dst, cores):
+def _first_hop(topo, src, dst, cores, s):
     a, b = (dst, dst) if topo.may_write(src, dst) else _relays(topo, src, dst, cores)
-    return (a, topo.engines(src, a)[0::2]), (b, topo.engines(src, b)[1::2])
+    if s == 1:
+        return (a, topo.engines(src, a)[0::2]), (b, topo.engines(src, b)[1::2])
+    return (a, topo.engines(src, a)), (b, topo.engines(src, b))
 
 
-def _arrival(topo, src, dst, cores):
+def _arrival(topo, src, dst, cores, s):
     if topo.may_write(src, dst):
-        (a, ea), (b, eb) = _first_hop(topo, src, dst, cores)
+        (a, ea), (b, eb) = _first_hop(topo, src, dst, cores, s)
         return len(ea) + len(eb)
     return sum(len(topo.engines(k, dst)) for k in _relays(topo, src, dst, cores))
 
@@ -81,7 +84,7 @@ def relay_program(g, core, T, topo):
         rid, pid = topo.addr(dst, core)
         sent = 0
         for s in range(1, H + 1):
-            g.wait_ge(T.sem["rl%d" % s], len(_first_hop(topo, src, dst, cores)[role][1]))
+            g.wait_ge(T.sem["rl%d" % s], len(_first_hop(topo, src, dst, cores, s)[role][1]))
             e = topo.engines(core, dst)
             if role == 0:
                 o, i = T["w%dc" % s][:, 256:320].bitcast(dt.uint8), T["r%dc" % s][:, 0:P].bitcast(dt.uint8)
@@ -120,25 +123,26 @@ def rank_program(g, core, T, topo):
         return E.matmul_mx(out[:, 0:k], T[l + "c"][:, la:la + 128], T[l + "s"][:, la:la + 128],
                            T[r + "c"][:, ra:ra + k], T[r + "s"][:, ra:ra + k], start, stop)
 
-    def send(s):
+    def pick_codes(o, a, b, i, c, d, off):
+        return V.tensor_copy(T[o + "c"][:, a:b].bitcast(dt.uint32), T[i + "c"][:, c:d].bitcast(dt.uint32).indirect(off))
+
+    def pick_scales(o, a, b, i, c, d, off):
+        return S.activation(T[o + "s"][:, a:b], T[i + "s"][:, c:d].indirect(off), ACT.Copy)
+
+    def send(s, codes, scales):
         name, a0 = SRC[s - 1]
-        (da, ea), (db, eb) = _first_hop(topo, core, nxt, cores)
+        (da, ea), (db, eb) = _first_hop(topo, core, nxt, cores, s)
         direct = da == nxt
         land, l0, sem = ("w%d" % s, 256, "arr%d" % s) if direct else ("r%d" % s, 0, "rl%d" % s)
         co, ci = T[land + "c"][:, l0:l0 + P].bitcast(dt.uint8), T[name + "c"][:, a0:a0 + P].bitcast(dt.uint8)
         (ra, pa), (rb, pb) = topo.addr(da, core), topo.addr(db, core)
-        if s == 1:
-            g.remote_dma(co, ci, T.sem[sem], T.sem.sent, pa, ra, _mask(ea))
-            g.remote_dma(T[land + "s"][:, l0:l0 + P], T[name + "s"][:, a0:a0 + P], T.sem[sem], T.sem.sent, pb, rb, _mask(eb))
-        else:
-            g.remote_dma_fused([
-                RemoteDMATransfer(dst_ids=[DstId(rid=ra, pnc=pa)], dma_engine_mask=_mask(ea), remote_sem=T.sem[sem], src=ci, dst=co),
-                RemoteDMATransfer(dst_ids=[DstId(rid=rb, pnc=pb)], dma_engine_mask=_mask(eb), remote_sem=T.sem[sem],
-                                  src=T[name + "s"][:, a0:a0 + PAD], dst=T[land + "s"][:, l0:l0 + PAD]),
-            ], local_sem=T.sem.sent)
+        w(g, codes)
+        g.remote_dma(co, ci, T.sem[sem], T.sem.sent, pa, ra, _mask(ea))
+        w(g, scales)
+        g.remote_dma(T[land + "s"][:, l0:l0 + P], T[name + "s"][:, a0:a0 + P], T.sem[sem], T.sem.sent, pb, rb, _mask(eb))
         cnt["sent"] = cnt.get("sent", 0) + len(ea) + len(eb)
 
-    cb, tt, qt, x1, x2, zz = T.cb, T.tt, T.qt, T.x1, T.x2, T.zz
+    cb, tt, qt, x1, x2, x3, zz, sp = T.cb, T.tt, T.qt, T.x1, T.x2, T.x3, T.zz, T.sp
     small = {"allow_small_or_imprecise_dtypes": True}
     low, up = slice(0, 64), slice(64, 128)
 
@@ -151,40 +155,39 @@ def rank_program(g, core, T, topo):
     sig(Y.dma_start(T.wt[:], T.w[:]), "lw", 16)
     sig(g.iota(T.di[:], [[1, 128]], 0, -1, **small), "g1")
     sig(g.iota(T.pi[:, 0:1], [[0, 1]], 0, 1), "g2")
-    sig(g.iota(T.iot[:], [[1, 64]], 64, 0, **small), "g3")
     sig(V.memset(T.pt[:, 256:512], 0.0), "a1")
     sig(V.memset(x2[:], 256.0), "a2")
-    sig(V.memset(tt[:], 0.0), "a2")
     sig(V.memset(cb[:, FP0:FM0], 0.0), "a2")
-    sig(V.memset(zz[:], 0.0), "a2")
-    w(V, "g1")
-    sig(V.tensor_scalar(T.rc[:], T.di[:], -65.0, -63.0, A.max, A.min), "a3")
     w(V, "a1", "lpn")
     sig(qz("k0", 0, 128, T.pt[:]), "qpn")
-    w(g, "qpn")
-    send(1)
+    send(1, "qpn", "qpn")
+    w(V, "g1")
+    sig(V.tensor_scalar(T.rc[:], T.di[:], -65.0, -63.0, A.max, A.min), "a3")
     sig(g.iota(T.d16[:], [[0, 8], [1, 16]], 0, -1, **small), "g4")
+    sig(g.iota(T.iot[:], [[1, 64]], 64, 0, **small), "g3")
     w(g, "a2")
     pat = [[0, 8], [1, 16], [16, 4]]
     sig(g.affine_select(x2[low, :], x2[low, :], pat, A.is_ge, 0.0, 0, -1), "g5")
     w(g, "g5")
     sig(g.affine_select(x2[low, :], x2[low, :], pat, A.not_equal, -256.0 * P, 0, -1), "g5")
     places(1)
-    w(S, "a3")
-    sig(S.activation(x1[:, 3:512:4], T.rc[:], ACT.Abs, bias=128.5, scale=2.0), "s3")
-    w(S, "lu")
+    w(S, "g1", "lu")
     for t in range(4):
         sig(S.activation(T.ur[:, t:512:4], T.di[:], ACT.Identity, bias=T.ut[:, t:t + 1], scale=0.0), "s1")
+    w(S, "a3")
+    sig(S.activation(x1[:, 3:512:4], T.rc[:], ACT.Abs, bias=128.5, scale=2.0), "s3")
     w(S, "s3")
     for t, f in ((0, ACT.Identity), (1, ACT.Identity), (2, ACT.Relu)):
         sig(S.activation(x1[:, t:512:4], x1[:, 3:512:4], f, bias=1.5, scale=-1.0), "s4")
     w(S, "s1")
     sig(S.activation(T.ur[:, 512:1024], T.ur[:, 0:512], ACT.Copy, scale=-1.0), "s1")
-    sig(V.memset(qt[:, QW:QW + 512], 0.0), "b2")
     w(V, "g2", "a2")
+    sig(V.tensor_scalar(cb[:, FP0 + 3:FP0 + 515:4], T.di[:], 0.0, None, A.is_equal), "b5")
     sig(V.tensor_scalar(T.pj[:, 0:1], T.pi[:, 0:1], 15, None, A.bitwise_and), "b0")
     sig(V.tensor_scalar(T.pj[:, 1:2], T.pi[:, 0:1], 112, None, A.bitwise_and), "b0")
-    sig(V.tensor_scalar(cb[:, FP0 + 3:FP0 + 515:4], T.di[:], 0.0, None, A.is_equal), "b5")
+    sig(V.memset(qt[:, QW:QW + 512], 0.0), "b2")
+    sig(V.memset(tt[:], 0.0), "b2")
+    sig(V.memset(zz[:], 0.0), "b2")
     w(S, "b5")
     sig(S.activation(cb[:, FM0:Z0], cb[:, FP0:FM0], ACT.Copy, scale=-0.5), "s2")
     w(V, "lx")
@@ -196,13 +199,13 @@ def rank_program(g, core, T, topo):
     sig(V.memset(zz[:, C:C + 1], -1.0), "b2")
     sig(V.memset(qt[64:65, QW + 10:QW + 58:12], float(P - G)), "b2")
     sig(V.memset(qt[64:65, QW + 11:QW + 59:12], 1.0), "b2")
-    sig(V.memset(T.dp[:, 0:12:3], -1e6), "b2")
-    sig(V.memset(T.dp[:, 1:12:3], 1e6), "b2")
-    w(V, "s4")
-    sig(qz("k1", 0, 128, x1[:]), "b3")
+    sig(V.memset(T.cs[:, 0:4], -16.0), "b2")
+    sig(V.memset(T.cs[:, 4:8], 16.0), "b2")
     w(V, "b5")
     for b in range(4):
         sig(qz(EB[b][0], EB[b][1], EB[b][1] + 128, cb[:, FP0 + 3 - b:FP0 + 515 - b]), "qe")
+    w(V, "s4")
+    sig(qz("k1", 0, 128, x1[:]), "b3")
     w(V, "s1")
     sig(qz("uq", 0, 256, T.ur[:]), "qu")
     w(V, "b0", "g3", "g4")
@@ -210,9 +213,12 @@ def rank_program(g, core, T, topo):
     w(S, "b1")
     sig(S.activation(x2[up, 0:512:4], T.mt[up, :], ACT.Copy), "s5")
     sig(S.activation(x2[up, 1:512:4], T.mt[up, :], ACT.Copy, scale=16.0), "s5")
+    w(S, "s2")
+    sig(S.activation(x3[:], cb[:, 0:512], ACT.Identity, bias=1.0, scale=0.0), "s6")
+    sig(S.activation(sp[:], cb[:, 0:4 * NT], ACT.Copy, scale=0.0), "s6")
     kk = T.iot[:, 0:64:16]
     sig(V.tensor_scalar(T.mk[:], kk, T.pf[:, 1:2], None, A.is_equal), "b4")
-    sig(V.tensor_scalar(T.dp[:, 2:12:3], kk, T.pf[:, 0:1], 64.0, A.add, A.add), "b4")
+    sig(V.tensor_scalar(T.dp[:], kk, T.pf[:, 0:1], 64.0, A.add, A.add), "b4")
     sig(V.tensor_scalar(T.pf[:, 2:3], T.pf[:, 0:1], -1024.0, 15360.0, A.mult, A.add), "b4")
     w(V, "s2")
     for b in range(4):
@@ -222,101 +228,142 @@ def rank_program(g, core, T, topo):
     w(V, "lw")
     sig(qz("wq", 0, 128, T.wt[:]), "qe")
     w(V, "qe", "b2", "b3", "b4")
-    w(S, "b2", "b4")
+    w(S, "b2", "b4", "s6")
     w(E, "qx", "qu")
     direct_in = topo.may_write(prv, core)
 
     for h in range(1, H + 1):
         Wn, Wx = "w%d" % h, "w%d" % (h + 1)
         an, a0 = SRC[h]
-        op, ot = T.offp[:, 4 * h:4 * h + 4], T.offt[:, 8 * h:8 * h + 8]
+        op, ot, on = T.offp[:, 4 * h:4 * h + 4], T.offt[:, 8 * h:8 * h + 8], T.offp[:, 0:4]
         iv = 192 * (h - 1)
+        last = h == H
 
         def ousted(b, Wn=Wn):
             mm(T["pz%d" % b], EB[b][0], EB[b][1], Wn, 192, True, False)
 
+        def entering(name, first):
+            for b in range(4):
+                sig(mm(T["pz%d" % b], FB[b][0], FB[b][1], name, first - 64, False, True), "tz%d" % b)
+
+        def z_tile(*bs):
+            for b in bs:
+                w(S, "tz%d" % b)
+                sig(S.activation(cb[:, Z0 + b:Q0:4], T["pz%d" % b][:, 64:128], ACT.Copy), "sz")
+
         late = h == (3 if direct_in else 2)
+        arrived = _arrival(topo, prv, core, cores, h)
+        if late:
+            E.wait_ge(T.sem["arr%d" % h], arrived)
+        if h > 1:
+            w(E, "c5")
         if not late:
             mm(T.pb, "uq", 0, Wn, 128, True, False)
-        E.wait_ge(T.sem["arr%d" % h], _arrival(topo, prv, core, cores))
+            E.wait_ge(T.sem["arr%d" % h], arrived)
         sig(mm(T.pa, Wn, 192, Wn, 128), "ts")
         if late:
             mm(T.pb, "uq", 0, Wn, 128, True, False)
         sig(mm(T.pb, Wn, 192, "uq", 128, False, True), "td")
         if h == 1:
             w(E, "qe", "b3")
+        else:
+            w(E, "sy")
         ousted(0)
         ousted(1)
-        if h == H:
+        if last:
             w(Y, "sy", "ts")
             sig(Y.dma_start(T.y[:, 0:P * (H - 1)], T.yy[:, 0:P * (H - 1)]), "st1", 16)
         top = T.pmx[up, 127:128]
         w(V, "ts")
         sig(V.tensor_tensor_scan(T.pmx[up, :], T.pa[up, 0:128], zz[up, 0:C], -1e29, A.max, A.add), "vs")
         w(V, "vs")
-        sig(V.tensor_scalar(tt[up, 0:512:4], T.pmx[up, :], top, 1.0, A.is_ge, A.subtract), "vt")
+        sig(V.tensor_scalar(tt[up, 0:512:4], T.pmx[up, :], top, 1.0, A.is_ge, A.subtract), "c1")
         w(S, "td")
-        sig(S.activation(tt[up, 2:512:4], T.pb[up, 0:128], ACT.Sign), "sf")
+        sig(S.activation(tt[up, 2:512:4], T.pb[up, 0:128], ACT.Sign), "c1")
         w(S, "vs")
-        sig(S.activation(tt[up, 5:512:4], T.pmx[up, 0:127], ACT.Sign, bias=top, scale=-1.0, accum_out=T.nm[up, 0:1]), "sh")
+        sig(S.activation(tt[up, 5:512:4], T.pmx[up, 0:127], ACT.Sign, bias=top, scale=-1.0, accum_out=T.nm[up, 0:1]), "c1")
         sig(S.activation(T.tmp[up, :], T.pmx[up, 15:128:16], ACT.Sign, bias=top, scale=-1.0, accum_out=T.nm[up, 1:2]), "shi")
-        w(V, "vt", "sf", "sh")
+        w(V, "c1")
         sig(qz("tq", 0, NT, tt[:]), "vq1")
         if h == 1:
             w(V, "g5", "s5")
-            sig(qz("k1", 192, 320, x2[:]), "b3")
+            sig(qz("k1", 192, 320, x2[:]), "b6")
         w(E, "vq1")
         sig(mm(T.pcc, "k1", 0, "tq", 0, k=NT), "tv")
         ousted(2)
-        w(S, "sh", "shi")
+        if h == 1:
+            w(E, "b6")
+        w(S, "c1", "shi")
+        if last:
+            sig(S.activation(sp[up, 0:20:5], T.cs[up, 0:4], ACT.Identity, bias=T.nm[up, 0:1], scale=T.nm[up, 1:2]), "c6")
+            sig(S.activation(sp[up, 16:36:5], T.cs[up, 4:8], ACT.Identity, scale=T.nm[up, 1:2]), "c6")
+            w(V, "c6")
+            sig(qz("sq", 0, NT, sp[:]), "vsp")
+            w(E, "b7", "vsp")
+            mm(T.pa, "k3", 0, "sq", 0, True, False)
+            sig(mm(T.pa, "k3", 0, "sq", 4, False, True), "tn")
         sig(S.activation(T.nm[up, 2:3], T.nm[up, 1:2], ACT.Identity, bias=T.nm[up, 0:1], scale=-16.0), "slo")
-        sig(S.activation(qt[up, QW + 5:QW + 53:12], T.mk[up, :], ACT.Identity, scale=T.nm[up, 1:2]), "sm")
+        sig(S.activation(qt[up, QW + 5:QW + 53:12], T.mk[up, :], ACT.Identity, scale=T.nm[up, 1:2]), "c2")
         w(S, "slo")
-        sig(S.activation(qt[up, QW + 4:QW + 52:12], T.mk[up, :], ACT.Identity, scale=T.nm[up, 2:3]), "sm")
+        sig(S.activation(qt[up, QW + 4:QW + 52:12], T.mk[up, :], ACT.Identity, scale=T.nm[up, 2:3]), "c2")
         w(V, "tv")
-        sig(V.tensor_tensor_scan(qt[low, 0:ST * NT:ST], T.pcc[low, 0:NT], zz[low, 0:NT], 1.0, A.max, A.add), "vr")
-        w(V, "vr", "sm")
+        sig(V.tensor_tensor_scan(qt[low, 0:ST * NT:ST], T.pcc[low, 0:NT], zz[low, 0:NT], 1.0, A.max, A.add), "c2")
+        w(V, "c2")
         sig(qz("qq", 0, 128, qt[:, QW:QW + 512]), "vq2")
-        w(E, "vq2", "b3")
+        w(E, "vq2")
         sig(mm(T.pd, "k1", 192, "qq", 0), "tm")
         ousted(3)
-        w(V, "tm")
-        sig(V.tensor_tensor_scan(T.st[:], T.pd[:, 0:12], T.dp[:], 0.0, A.max, A.min), "vg")
-        w(V, "vg")
-        sig(V.tensor_copy(op, T.st[:, 2:12:3]), "vo")
+        if last:
+            w(V, "tn")
+            sig(V.tensor_copy(on, T.pa[:, 0:4]), "vn")
+            w(V, "vn")
+            w(S, "vn")
+            sig(pick_codes("k3", E0, E0 + P, Wn, 128, 256, on), "c7")
+            sig(pick_scales("k3", E0, E0 + P, Wn, 128, 256, on), "c7")
+            w(E, "c7")
+            entering("k3", E0)
+            z_tile(0)
+        w(V, "g6", "tm")
+        for c in range(4):
+            sig(V.tensor_scalar(T.offp[:, 4 * h + c:4 * h + c + 1], T.pd[:, 3 * c + 1:3 * c + 2], T.pd[:, 3 * c + 2:3 * c + 3],
+                                T.dp[:, c:c + 1], A.max, A.min), "vo")
         w(V, "vo")
         w(S, "vo")
-        sig(V.tensor_copy(T[an + "c"][:, a0:a0 + P].bitcast(dt.uint32), T[Wn + "c"][:, 128:320].bitcast(dt.uint32).indirect(op)), "va")
-        sig(S.activation(T[an + "s"][:, a0:a0 + P], T[Wn + "s"][:, 128:320].indirect(op), ACT.Copy), "sa")
-        w(V, "g6")
-        if h < H:
-            w(g, "va", "sa")
-            if h == 1:
-                w(g, "b3")
-            send(h + 1)
+        if last:
+            sig(V.tensor_copy(T.inv[:, iv:iv + 192].indirect(op), T.iot[:]), "vi")
+        sig(pick_codes(an, a0, a0 + P, Wn, 128, 320, op), "va")
+        sig(pick_scales(an, a0, a0 + P, Wn, 128, 320, op), "sa")
+        if not last:
+            send(h + 1, "va", "sa")
             places(h + 1)
-        sig(V.tensor_copy(T.inv[:, iv:iv + 192].indirect(op), T.iot[:]), "vi")
+            sig(V.tensor_copy(T.inv[:, iv:iv + 192].indirect(op), T.iot[:]), "vi")
+        if h == 1:
+            w(g, "s6")
+            sig(g.affine_select(x3[:], x3[:], pat, A.is_equal, 0.0, 64, -1), "g7")
         w(E, "va", "sa")
-        for b in range(4):
-            sig(mm(T["pz%d" % b], FB[b][0], FB[b][1], an, a0 - 64, False, True), "tz%d" % b)
+        if not last:
+            entering(an, a0)
         sig(mm(T.pcc, "wq", 0, an, a0 - 64), "ty")
+        z_tile(*range(1 if last else 0, 4))
         w(V, "vi")
         sig(V.tensor_tensor_scan(T.stt[:], T.dt2[:], T.inv[:, iv:iv + 128], 0.0, A.add, A.max), "vst")
+        if last:
+            w(V, "sz")
+            sig(qz(Wn, 0, 128, cb[:, ZP:Q0]), "c4")
         w(V, "vst")
-        sig(V.tensor_scalar(ot, T.stt[:, 15:128:16], T.pf[:, 2:3], None, A.subtract), "vot")
-        for b in range(4):
-            w(S, "tz%d" % b)
-            sig(S.activation(cb[:, Z0 + b:Q0:4], T["pz%d" % b][:, 64:128], ACT.Copy), "sz")
+        sig(V.tensor_scalar(ot, T.stt[:, 15:128:16], T.pf[:, 2:3], None, A.subtract), "c4")
         w(S, "ty")
         sig(S.activation(T.yy[:, P * (h - 1):P * h], T.pcc[:, 64:128], ACT.Copy), "sy")
-        w(V, "sz")
-        sig(qz(Wn, 0, 128, cb[:, ZP:Q0]), "vqz")
-        w(V, "vqz", "vot")
-        w(S, "vqz", "vot")
-        sig(V.tensor_copy(T[Wx + "c"][:, 128:256].bitcast(dt.uint32), T[Wn + "c"][:, 0:256].bitcast(dt.uint32).indirect(ot)), "vb")
-        sig(S.activation(T[Wx + "s"][:, 128:256], T[Wn + "s"][:, 0:256].indirect(ot), ACT.Copy), "sb")
-        if h < H:
-            w(E, "sy", "vb", "sb")
+        if not last:
+            w(V, "sz")
+            sig(qz(Wn, 0, 128, cb[:, ZP:Q0]), "c4")
+        w(V, "c4")
+        w(S, "c4")
+        sig(pick_codes(Wx, 128, 256, Wn, 0, 256, ot), "vb" if last else "c5")
+        sig(pick_scales(Wx, 128, 256, Wn, 0, 256, ot), "sb" if last else "c5")
+        if h == 2:
+            w(V, "g7")
+            sig(qz("k3", 0, 128, x3[:]), "b7")
 
     an, a0 = SRC[H]
     w(Y, "va")

from concourse.bass import DstId, RemoteDMATransfer
from concourse.mybir import dt, AluOpType, AxisListType, ActivationFunctionType

P, C, G, H = 64, 128, 16, 3
X4, U8, BF, F32 = "float8_e4m3fn_x4", "uint8", "bfloat16", "float32"
FP0, FM0, ZP, Z0, Q0 = 0, 520, 784, 1040, 1296
SRC = [("k0", 0), ("k1", 128), ("k2", 128), ("k3", 576)]
EB = [("k0", 128), ("k2", 0), ("k2", 192), ("k1", 320)]
FB = [("k2", 320), ("k3", 192), ("k3", 320), ("k3", 448)]
E0 = 128
NT = C + 4
ST = 13
QW = ST * C - 8

SCRATCH = {
    "cb": ("sbuf", [128, Q0], BF), "pt": ("sbuf", [128, 512], BF), "xt": ("sbuf", [128, 512], BF),
    "wt": ("sbuf", [128, 512], BF), "ut": ("sbuf", [128, 8], BF), "ur": ("sbuf", [128, 1024], BF),
    "tt": ("sbuf", [128, 4 * NT], BF), "x1": ("sbuf", [128, 512], BF), "x2": ("sbuf", [128, 512], BF),
    "x3": ("sbuf", [128, 512], BF), "sp": ("sbuf", [128, 4 * NT], BF), "cs": ("sbuf", [128, 8], F32),
    "qt": ("sbuf", [128, QW + 512], BF), "mt": ("sbuf", [128, 128], BF), "zz": ("sbuf", [128, 136], BF),
    "di": ("sbuf", [128, 128], F32), "d16": ("sbuf", [128, 128], F32), "rc": ("sbuf", [128, 128], F32),
    "pi": ("sbuf", [128, 4], "int32"), "mk": ("sbuf", [128, 4], F32),
    "pj": ("sbuf", [128, 4], "int32"), "pf": ("sbuf", [128, 4], F32), "iot": ("sbuf", [128, 64], F32),
    "inv": ("sbuf", [128, 576], F32), "tmp": ("sbuf", [128, 8], F32), "dp": ("sbuf", [128, 4], F32),
    "dt2": ("sbuf", [128, 128], F32), "nm": ("sbuf", [128, 4], F32), "pmx": ("sbuf", [128, 128], F32),
    "stt": ("sbuf", [128, 128], F32),
    "offp": ("sbuf", [128, 16], "uint16"), "offt": ("sbuf", [128, 32], "uint16"), "yy": ("sbuf", [128, 192], F32),
    "pa": ("psum", [128, 512], F32), "pb": ("psum", [128, 512], F32), "pcc": ("psum", [128, 512], F32),
    "pd": ("psum", [128, 512], F32),
}
for _b in range(4):
    SCRATCH["pz%d" % _b] = ("psum", [128, 512], F32)
for _n, _w in (("k0", 256), ("k1", 448), ("k2", 448), ("k3", 640), ("wq", 128), ("uq", 256), ("tq", NT), ("qq", 128),
               ("sq", NT), ("w1", 320), ("w2", 320), ("w3", 320), ("w4", 256), ("r1", 64), ("r2", 64), ("r3", 64)):
    SCRATCH[_n + "c"] = ("sbuf", [128, _w], X4)
    SCRATCH[_n + "s"] = ("sbuf", [128, _w], U8)

SEMAPHORES = ["lpn", "lx", "lu", "lw", "g1", "g2", "g3", "g4", "g5", "g6", "g7", "a1", "a2", "a3", "qpn", "qx", "qu", "b0",
              "b1", "b2", "b3", "b4", "b5", "b6", "b7", "qe", "s1", "s2", "s3", "s4", "s5", "s6", "arr1", "arr2", "arr3",
              "rl1", "rl2", "rl3", "sent", "ts", "td", "tv", "tm", "tn", "tz0", "tz1", "tz2", "tz3", "ty",
              "vs", "c1", "vq1", "c2", "vq2", "vo", "va", "sa", "vi", "vst", "c4", "c5", "c6", "c7", "vsp", "vn", "vb",
              "shi", "slo", "sz", "sy", "sb", "st1", "st2"]


def _mask(engines):
    m = 0
    for e in engines:
        m |= 1 << e
    return m


def _relays(topo, src, dst, cores):
    c = [k for k in topo.cores_of(src) if k not in cores and topo.may_write(k, dst)]
    same = [k for k in c if topo.die(k) == topo.die(src)]
    other = [k for k in c if topo.die(k) != topo.die(src)]
    return [same[0], other[0]] if same and other else c[:2]


def _first_hop(topo, src, dst, cores, s):
    a, b = (dst, dst) if topo.may_write(src, dst) else _relays(topo, src, dst, cores)
    if s == 1:
        return (a, topo.engines(src, a)[0::2]), (b, topo.engines(src, b)[1::2])
    return (a, topo.engines(src, a)), (b, topo.engines(src, b))


def _arrival(topo, src, dst, cores, s):
    if topo.may_write(src, dst):
        (a, ea), (b, eb) = _first_hop(topo, src, dst, cores, s)
        return len(ea) + len(eb)
    return sum(len(topo.engines(k, dst)) for k in _relays(topo, src, dst, cores))


def relay_program(g, core, T, topo):
    cores = list(T.cores)
    n = len(cores)
    for r in range(n):
        src, dst = cores[r], cores[(r + 1) % n]
        if topo.may_write(src, dst):
            continue
        rel = _relays(topo, src, dst, cores)
        if core not in rel:
            continue
        role = rel.index(core)
        rid, pid = topo.addr(dst, core)
        sent = 0
        for s in range(1, H + 1):
            g.wait_ge(T.sem["rl%d" % s], len(_first_hop(topo, src, dst, cores, s)[role][1]))
            e = topo.engines(core, dst)
            if role == 0:
                o, i = T["w%dc" % s][:, 256:320].bitcast(dt.uint8), T["r%dc" % s][:, 0:P].bitcast(dt.uint8)
            else:
                o, i = T["w%ds" % s][:, 256:320], T["r%ds" % s][:, 0:P]
            g.remote_dma(o, i, T.sem["arr%d" % s], T.sem.sent, pid, rid, _mask(e))
            sent += len(e)
        g.wait_ge(T.sem.sent, sent)


def rank_program(g, core, T, topo):
    rank = T.rank_of(core)
    if rank is None:
        relay_program(g, core, T, topo)
        return
    cores = list(T.cores)
    n = len(cores)
    nxt, prv = cores[(rank + 1) % n], cores[(rank - 1) % n]
    V, S, E, Y = g.vector, g.scalar, g.tensor, g.sync
    A, ACT = AluOpType, ActivationFunctionType
    cnt, seen = {}, {}

    def sig(ins, name, k=1):
        ins.then_inc(T.sem[name], k)
        cnt[name] = cnt.get(name, 0) + k

    def w(q, *names):
        for nm in names:
            q.wait_ge(T.sem[nm], cnt[nm])
            seen[nm] = cnt[nm]

    def qz(name, a, b, src):
        return V.quantize_mx(T[name + "c"][:, a:b], T[name + "s"][:, a:b], src)

    def mm(out, l, la, r, ra, start=True, stop=True, k=128):
        return E.matmul_mx(out[:, 0:k], T[l + "c"][:, la:la + 128], T[l + "s"][:, la:la + 128],
                           T[r + "c"][:, ra:ra + k], T[r + "s"][:, ra:ra + k], start, stop)

    def pick_codes(o, a, b, i, c, d, off):
        return V.tensor_copy(T[o + "c"][:, a:b].bitcast(dt.uint32), T[i + "c"][:, c:d].bitcast(dt.uint32).indirect(off))

    def pick_scales(o, a, b, i, c, d, off):
        return S.activation(T[o + "s"][:, a:b], T[i + "s"][:, c:d].indirect(off), ACT.Copy)

    def send(s, codes, scales):
        name, a0 = SRC[s - 1]
        (da, ea), (db, eb) = _first_hop(topo, core, nxt, cores, s)
        direct = da == nxt
        land, l0, sem = ("w%d" % s, 256, "arr%d" % s) if direct else ("r%d" % s, 0, "rl%d" % s)
        co, ci = T[land + "c"][:, l0:l0 + P].bitcast(dt.uint8), T[name + "c"][:, a0:a0 + P].bitcast(dt.uint8)
        (ra, pa), (rb, pb) = topo.addr(da, core), topo.addr(db, core)
        w(g, codes)
        g.remote_dma(co, ci, T.sem[sem], T.sem.sent, pa, ra, _mask(ea))
        w(g, scales)
        g.remote_dma(T[land + "s"][:, l0:l0 + P], T[name + "s"][:, a0:a0 + P], T.sem[sem], T.sem.sent, pb, rb, _mask(eb))
        cnt["sent"] = cnt.get("sent", 0) + len(ea) + len(eb)

    cb, tt, qt, x1, x2, x3, zz, sp = T.cb, T.tt, T.qt, T.x1, T.x2, T.x3, T.zz, T.sp
    small = {"allow_small_or_imprecise_dtypes": True}
    low, up = slice(0, 64), slice(64, 128)

    def places(h):
        sig(g.iota(T.inv[:, 192 * (h - 1):192 * (h - 1) + C], [[1, C]], C, 0, **small), "g6")

    sig(Y.dma_start(T.pt[:, 0:256], T.pn[:]), "lpn", 16)
    sig(Y.dma_start(T.xt[:], T.x[:]), "lx", 16)
    sig(Y.dma_start(T.ut[:, 0:4], T.u[:]), "lu", 16)
    sig(Y.dma_start(T.wt[:], T.w[:]), "lw", 16)
    sig(g.iota(T.di[:], [[1, 128]], 0, -1, **small), "g1")
    sig(g.iota(T.pi[:, 0:1], [[0, 1]], 0, 1), "g2")
    sig(V.memset(T.pt[:, 256:512], 0.0), "a1")
    sig(V.memset(x2[:], 256.0), "a2")
    sig(V.memset(cb[:, FP0:FM0], 0.0), "a2")
    w(V, "a1", "lpn")
    sig(qz("k0", 0, 128, T.pt[:]), "qpn")
    send(1, "qpn", "qpn")
    w(V, "g1")
    sig(V.tensor_scalar(T.rc[:], T.di[:], -65.0, -63.0, A.max, A.min), "a3")
    sig(g.iota(T.d16[:], [[0, 8], [1, 16]], 0, -1, **small), "g4")
    sig(g.iota(T.iot[:], [[1, 64]], 64, 0, **small), "g3")
    w(g, "a2")
    pat = [[0, 8], [1, 16], [16, 4]]
    sig(g.affine_select(x2[low, :], x2[low, :], pat, A.is_ge, 0.0, 0, -1), "g5")
    w(g, "g5")
    sig(g.affine_select(x2[low, :], x2[low, :], pat, A.not_equal, -256.0 * P, 0, -1), "g5")
    places(1)
    w(S, "g1", "lu")
    for t in range(4):
        sig(S.activation(T.ur[:, t:512:4], T.di[:], ACT.Identity, bias=T.ut[:, t:t + 1], scale=0.0), "s1")
    w(S, "a3")
    sig(S.activation(x1[:, 3:512:4], T.rc[:], ACT.Abs, bias=128.5, scale=2.0), "s3")
    w(S, "s3")
    for t, f in ((0, ACT.Identity), (1, ACT.Identity), (2, ACT.Relu)):
        sig(S.activation(x1[:, t:512:4], x1[:, 3:512:4], f, bias=1.5, scale=-1.0), "s4")
    w(S, "s1")
    sig(S.activation(T.ur[:, 512:1024], T.ur[:, 0:512], ACT.Copy, scale=-1.0), "s1")
    w(V, "g2", "a2")
    sig(V.tensor_scalar(cb[:, FP0 + 3:FP0 + 515:4], T.di[:], 0.0, None, A.is_equal), "b5")
    sig(V.tensor_scalar(T.pj[:, 0:1], T.pi[:, 0:1], 15, None, A.bitwise_and), "b0")
    sig(V.tensor_scalar(T.pj[:, 1:2], T.pi[:, 0:1], 112, None, A.bitwise_and), "b0")
    sig(V.memset(qt[:, QW:QW + 512], 0.0), "b2")
    sig(V.memset(tt[:], 0.0), "b2")
    sig(V.memset(zz[:], 0.0), "b2")
    w(S, "b5")
    sig(S.activation(cb[:, FM0:Z0], cb[:, FP0:FM0], ACT.Copy, scale=-0.5), "s2")
    w(V, "lx")
    sig(qz("w1", 128, 256, T.xt[:]), "qx")
    w(V, "b0", "b2")
    sig(V.tensor_copy(T.pf[:, 0:2], T.pj[:, 0:2]), "b0")
    sig(V.tensor_scalar(T.pf[:, 3:4], T.pj[:, 1:2], -1.0, None, A.mult), "b0")
    sig(V.memset(tt[up, 1:2], 1.0), "b2")
    sig(V.memset(zz[:, C:C + 1], -1.0), "b2")
    sig(V.memset(qt[64:65, QW + 10:QW + 58:12], float(P - G)), "b2")
    sig(V.memset(qt[64:65, QW + 11:QW + 59:12], 1.0), "b2")
    sig(V.memset(T.cs[:, 0:4], -16.0), "b2")
    sig(V.memset(T.cs[:, 4:8], 16.0), "b2")
    w(V, "b5")
    for b in range(4):
        sig(qz(EB[b][0], EB[b][1], EB[b][1] + 128, cb[:, FP0 + 3 - b:FP0 + 515 - b]), "qe")
    w(V, "s4")
    sig(qz("k1", 0, 128, x1[:]), "b3")
    w(V, "s1")
    sig(qz("uq", 0, 256, T.ur[:]), "qu")
    w(V, "b0", "g3", "g4")
    sig(V.tensor_scalar(T.mt[:], T.d16[:], T.pf[:, 3:4], None, A.is_equal), "b1")
    w(S, "b1")
    sig(S.activation(x2[up, 0:512:4], T.mt[up, :], ACT.Copy), "s5")
    sig(S.activation(x2[up, 1:512:4], T.mt[up, :], ACT.Copy, scale=16.0), "s5")
    w(S, "s2")
    sig(S.activation(x3[:], cb[:, 0:512], ACT.Identity, bias=1.0, scale=0.0), "s6")
    sig(S.activation(sp[:], cb[:, 0:4 * NT], ACT.Copy, scale=0.0), "s6")
    kk = T.iot[:, 0:64:16]
    sig(V.tensor_scalar(T.mk[:], kk, T.pf[:, 1:2], None, A.is_equal), "b4")
    sig(V.tensor_scalar(T.dp[:], kk, T.pf[:, 0:1], 64.0, A.add, A.add), "b4")
    sig(V.tensor_scalar(T.pf[:, 2:3], T.pf[:, 0:1], -1024.0, 15360.0, A.mult, A.add), "b4")
    w(V, "s2")
    for b in range(4):
        sig(qz(FB[b][0], FB[b][1], FB[b][1] + 128, cb[:, FM0 + 3 - b:FM0 + 515 - b]), "qe")
    w(V, "b1")
    sig(V.tensor_scalar(T.dt2[:], T.mt[:], -1048576.0, 1024.0, A.mult, A.add), "b4")
    w(V, "lw")
    sig(qz("wq", 0, 128, T.wt[:]), "qe")
    w(V, "qe", "b2", "b3", "b4")
    w(S, "b2", "b4", "s6")
    w(E, "qx", "qu")
    direct_in = topo.may_write(prv, core)

    for h in range(1, H + 1):
        Wn, Wx = "w%d" % h, "w%d" % (h + 1)
        an, a0 = SRC[h]
        op, ot, on = T.offp[:, 4 * h:4 * h + 4], T.offt[:, 8 * h:8 * h + 8], T.offp[:, 0:4]
        iv = 192 * (h - 1)
        last = h == H

        def ousted(b, Wn=Wn):
            mm(T["pz%d" % b], EB[b][0], EB[b][1], Wn, 192, True, False)

        def entering(name, first):
            for b in range(4):
                sig(mm(T["pz%d" % b], FB[b][0], FB[b][1], name, first - 64, False, True), "tz%d" % b)

        def z_tile(*bs):
            for b in bs:
                w(S, "tz%d" % b)
                sig(S.activation(cb[:, Z0 + b:Q0:4], T["pz%d" % b][:, 64:128], ACT.Copy), "sz")

        late = h == (3 if direct_in else 2)
        arrived = _arrival(topo, prv, core, cores, h)
        if late:
            E.wait_ge(T.sem["arr%d" % h], arrived)
        if h > 1:
            w(E, "c5")
        if not late:
            mm(T.pb, "uq", 0, Wn, 128, True, False)
            E.wait_ge(T.sem["arr%d" % h], arrived)
        sig(mm(T.pa, Wn, 192, Wn, 128), "ts")
        if late:
            mm(T.pb, "uq", 0, Wn, 128, True, False)
        sig(mm(T.pb, Wn, 192, "uq", 128, False, True), "td")
        if h == 1:
            w(E, "qe", "b3")
        else:
            w(E, "sy")
        ousted(0)
        ousted(1)
        if last:
            w(Y, "sy", "ts")
            sig(Y.dma_start(T.y[:, 0:P * (H - 1)], T.yy[:, 0:P * (H - 1)]), "st1", 16)
        top = T.pmx[up, 127:128]
        w(V, "ts")
        sig(V.tensor_tensor_scan(T.pmx[up, :], T.pa[up, 0:128], zz[up, 0:C], -1e29, A.max, A.add), "vs")
        w(V, "vs")
        sig(V.tensor_scalar(tt[up, 0:512:4], T.pmx[up, :], top, 1.0, A.is_ge, A.subtract), "c1")
        w(S, "td")
        sig(S.activation(tt[up, 2:512:4], T.pb[up, 0:128], ACT.Sign), "c1")
        w(S, "vs")
        sig(S.activation(tt[up, 5:512:4], T.pmx[up, 0:127], ACT.Sign, bias=top, scale=-1.0, accum_out=T.nm[up, 0:1]), "c1")
        sig(S.activation(T.tmp[up, :], T.pmx[up, 15:128:16], ACT.Sign, bias=top, scale=-1.0, accum_out=T.nm[up, 1:2]), "shi")
        w(V, "c1")
        sig(qz("tq", 0, NT, tt[:]), "vq1")
        if h == 1:
            w(V, "g5", "s5")
            sig(qz("k1", 192, 320, x2[:]), "b6")
        w(E, "vq1")
        sig(mm(T.pcc, "k1", 0, "tq", 0, k=NT), "tv")
        ousted(2)
        if h == 1:
            w(E, "b6")
        w(S, "c1", "shi")
        if last:
            sig(S.activation(sp[up, 0:20:5], T.cs[up, 0:4], ACT.Identity, bias=T.nm[up, 0:1], scale=T.nm[up, 1:2]), "c6")
            sig(S.activation(sp[up, 16:36:5], T.cs[up, 4:8], ACT.Identity, scale=T.nm[up, 1:2]), "c6")
            w(V, "c6")
            sig(qz("sq", 0, NT, sp[:]), "vsp")
            w(E, "b7", "vsp")
            mm(T.pa, "k3", 0, "sq", 0, True, False)
            sig(mm(T.pa, "k3", 0, "sq", 4, False, True), "tn")
        sig(S.activation(T.nm[up, 2:3], T.nm[up, 1:2], ACT.Identity, bias=T.nm[up, 0:1], scale=-16.0), "slo")
        sig(S.activation(qt[up, QW + 5:QW + 53:12], T.mk[up, :], ACT.Identity, scale=T.nm[up, 1:2]), "c2")
        w(S, "slo")
        sig(S.activation(qt[up, QW + 4:QW + 52:12], T.mk[up, :], ACT.Identity, scale=T.nm[up, 2:3]), "c2")
        w(V, "tv")
        sig(V.tensor_tensor_scan(qt[low, 0:ST * NT:ST], T.pcc[low, 0:NT], zz[low, 0:NT], 1.0, A.max, A.add), "c2")
        w(V, "c2")
        sig(qz("qq", 0, 128, qt[:, QW:QW + 512]), "vq2")
        w(E, "vq2")
        sig(mm(T.pd, "k1", 192, "qq", 0), "tm")
        ousted(3)
        if last:
            w(V, "tn")
            sig(V.tensor_copy(on, T.pa[:, 0:4]), "vn")
            w(V, "vn")
            w(S, "vn")
            sig(pick_codes("k3", E0, E0 + P, Wn, 128, 256, on), "c7")
            sig(pick_scales("k3", E0, E0 + P, Wn, 128, 256, on), "c7")
            w(E, "c7")
            entering("k3", E0)
            z_tile(0)
        w(V, "g6", "tm")
        for c in range(4):
            sig(V.tensor_scalar(T.offp[:, 4 * h + c:4 * h + c + 1], T.pd[:, 3 * c + 1:3 * c + 2], T.pd[:, 3 * c + 2:3 * c + 3],
                                T.dp[:, c:c + 1], A.max, A.min), "vo")
        w(V, "vo")
        w(S, "vo")
        if last:
            sig(V.tensor_copy(T.inv[:, iv:iv + 192].indirect(op), T.iot[:]), "vi")
        sig(pick_codes(an, a0, a0 + P, Wn, 128, 320, op), "va")
        sig(pick_scales(an, a0, a0 + P, Wn, 128, 320, op), "sa")
        if not last:
            send(h + 1, "va", "sa")
            places(h + 1)
            sig(V.tensor_copy(T.inv[:, iv:iv + 192].indirect(op), T.iot[:]), "vi")
        if h == 1:
            w(g, "s6")
            sig(g.affine_select(x3[:], x3[:], pat, A.is_equal, 0.0, 64, -1), "g7")
        w(E, "va", "sa")
        if not last:
            entering(an, a0)
        sig(mm(T.pcc, "wq", 0, an, a0 - 64), "ty")
        z_tile(*range(1 if last else 0, 4))
        w(V, "vi")
        sig(V.tensor_tensor_scan(T.stt[:], T.dt2[:], T.inv[:, iv:iv + 128], 0.0, A.add, A.max), "vst")
        if last:
            w(V, "sz")
            sig(qz(Wn, 0, 128, cb[:, ZP:Q0]), "c4")
        w(V, "vst")
        sig(V.tensor_scalar(ot, T.stt[:, 15:128:16], T.pf[:, 2:3], None, A.subtract), "c4")
        w(S, "ty")
        sig(S.activation(T.yy[:, P * (h - 1):P * h], T.pcc[:, 64:128], ACT.Copy), "sy")
        if not last:
            w(V, "sz")
            sig(qz(Wn, 0, 128, cb[:, ZP:Q0]), "c4")
        w(V, "c4")
        w(S, "c4")
        sig(pick_codes(Wx, 128, 256, Wn, 0, 256, ot), "vb" if last else "c5")
        sig(pick_scales(Wx, 128, 256, Wn, 0, 256, ot), "sb" if last else "c5")
        if h == 2:
            w(V, "g7")
            sig(qz("k3", 0, 128, x3[:]), "b7")

    an, a0 = SRC[H]
    w(Y, "va")
    sig(Y.dma_start(T.pc[:], T[an + "c"][:, a0:a0 + P].bitcast(dt.uint8)), "st1", 16)
    w(Y, "sa")
    for k in range(4):
        sig(Y.dma_start(T.psc[4 * k:4 * k + 4, :], T[an + "s"][32 * k:32 * k + 4, a0:a0 + P]), "st1", 16)
    w(Y, "sy")
    sig(Y.dma_start(T.y[:, P * (H - 1):P * H], T.yy[:, P * (H - 1):P * H]), "st1", 16)
    w(Y, "vb")
    sig(Y.dma_start(T.oc[:], T.w4c[:, 128:256].bitcast(dt.uint8)), "st1", 16)
    w(Y, "sb")
    w(S, "sb")
    for k in range(4):
        sig((Y if k == 3 else S).dma_start(T.osc[4 * k:4 * k + 4, :], T.w4s[32 * k:32 * k + 4, 128:256]), "st1" if k == 3 else "st2", 16)
    w(Y, "st1")
    w(S, "st2")
    for nm in cnt:
        if seen.get(nm, 0) < cnt[nm]:
            w(g, nm)
